import numpy as np
import ml_dtypes


def mxq(x, axis, fmt="e4m3"):
    dtype, down = {"e4m3": (ml_dtypes.float8_e4m3fn, 7), "e5m2": (ml_dtypes.float8_e5m2, 14)}[fmt]
    v = np.moveaxis(np.asarray(x, np.float32).astype(ml_dtypes.bfloat16).astype(np.float64), axis, -1)
    blocks = v.reshape(v.shape[:-1] + (-1, 32))
    amax = np.abs(blocks).max(-1, keepdims=True)
    byte = np.maximum(np.where(amax > 0, np.frexp(amax)[1] - 1 + 127, 0) - down, 1)
    scale = np.exp2(byte - 127.0)
    codes = (blocks / scale).astype(np.float32).astype(dtype).astype(np.float64)
    return np.moveaxis((codes * scale).reshape(v.shape), -1, axis)


WIDE = False


def mx_kscale(k):
    if not WIDE:
        return np.ones(k)
    levels = np.array([10, -10, 5, -5, 0])
    if k % 512:
        return np.exp2(np.random.permutation(np.resize(levels, k // 32))).repeat(32)
    a = np.empty((k // 512, 16))
    for p in range(k // 512):
        a[p, :8] = np.random.permutation(np.resize(levels, 8))
        for g in range(8):
            far = levels[np.abs(levels - a[p, g]) >= 10]
            a[p, g + 8] = far[np.random.randint(len(far))]
    return np.exp2(a.ravel()).repeat(32)


def f64(x):
    return np.asarray(x).astype(np.float64)


def striped(idx):
    return np.tile(idx.reshape(-1, 16).T, (8, 1)).astype(np.uint16)


def unstriped(offs):
    return offs[:16].T.reshape(-1).astype(np.int64)


E2M1 = np.array([0.0, 0.5, 1.0, 1.5, 2.0, 3.0, 4.0, 6.0, -0.0, -0.5, -1.0, -1.5, -2.0, -3.0, -4.0, -6.0])


def pack_weight(w, fmt):
    k, n = w.shape
    w = f64(np.asarray(w, np.float32).astype(ml_dtypes.bfloat16)).reshape(k // 32, 32, n)
    amax = np.abs(w).max(1)
    if fmt == "e4m3":
        byte = np.frexp(amax)[1] - 1 + 127 - 7
    else:
        mant, ex = np.frexp(amax / 6.0)
        byte = np.where(mant > 0.5, ex, ex - 1) + 127
    byte = np.clip(np.where(amax > 0, byte, 1), 1, 254)
    scaled = (w * np.exp2(127.0 - byte)[:, None, :]).reshape(k, n).astype(np.float32)
    by_word = np.ascontiguousarray(scaled.reshape(k // 512, 128, 4, n).transpose(0, 1, 3, 2))
    if fmt == "e4m3":
        words = by_word.astype(ml_dtypes.float8_e4m3fn).view(np.uint8)
    else:
        c = by_word.astype(ml_dtypes.float4_e2m1fn).view(np.uint8) & 0xF
        words = (c[..., 0::2] | (c[..., 1::2] << 4)).reshape(k // 512, 128, 2 * n)
    return np.ascontiguousarray(words), np.ascontiguousarray(byte.astype(np.uint8).reshape(k // 512, 16, n))


def unpack_weight(words, scales, fmt):
    g, _, n = scales.shape
    words = np.ascontiguousarray(words).reshape(g, 128, n, -1)
    if fmt == "e4m3":
        vals = words.view(ml_dtypes.float8_e4m3fn).astype(np.float64)
    else:
        nib = np.empty((g, 128, n, 4), np.uint8)
        nib[..., 0::2] = words & 0xF
        nib[..., 1::2] = words >> 4
        vals = E2M1[nib]
    vals = vals * np.repeat(np.exp2(scales.astype(np.float64) - 127.0), 8, axis=1)[..., None]
    return vals.transpose(0, 1, 3, 2).reshape(g * 512, n)


def silu(v):
    return v / (1.0 + np.exp(-np.maximum(v, -700.0)))


K, M, T, S = 1536, 1024, 2048, 1024


def setup_inputs():
    n = np.random.standard_normal
    s = mx_kscale(K)[:, None]
    u = mx_kscale(512)[:, None]
    v = pack_weight(n((K, T)) * s, "e4m3")
    p_w4 = pack_weight(n((K, M)) / np.sqrt(K) / s, "e2m1")
    return {
        "tab_words": v[0],
        "tab_scales": v[1],
        "w4_words": p_w4[0],
        "w4_scales": p_w4[1],
        "down": (n((K, 512)) / np.sqrt(K) / s * u.T).astype(np.float32),
        "up": (0.5 * n((512, M)) / np.sqrt(512) / u).astype(np.float32),
        "gT": n((M, T)).astype(np.float32),
        "b": (0.3 * n(1024)).astype(np.float32),
        "offs": striped(np.random.permutation(T)[:S]),
    }


def reference(tab_words, tab_scales, w4_words, w4_scales, down, up, gT, b, offs):
    tab_ = unpack_weight(tab_words, tab_scales, "e4m3")[:, unstriped(offs)]
    w4_ = unpack_weight(w4_words, w4_scales, "e2m1")
    down_ = mxq(f64(down), 0, "e4m3")
    up_ = mxq(f64(up), 0, "e4m3")
    h_ = mxq(down_.T @ tab_, 0, "e4m3")
    y = w4_.T @ tab_ + up_.T @ h_
    return (silu(y + f64(b)[:, None])) * f64(gT)[:, unstriped(offs)]

@@ -1,0 +1,269 @@
+from contextlib import ExitStack
+
+import concourse.mybir as mybir
+from concourse.masks import make_identity
+
+K, M, T, S, R = 1536, 1024, 2048, 1024, 512
+FLOPS = 2 * S * (K * R + K * M + R * M)
+
+F32 = mybir.dt.float32
+BF16 = mybir.dt.bfloat16
+I32 = mybir.dt.int32
+U32 = mybir.dt.uint32
+U16 = mybir.dt.uint16
+U8 = mybir.dt.uint8
+FP8X4 = mybir.dt.float8_e4m3fn_x4
+FP4X4 = mybir.dt.float4_e2m1fn_x4
+MULT = mybir.AluOpType.mult
+SILU = mybir.ActivationFunctionType.Silu
+
+P = 128
+PACK = 4
+K_PASS = P * PACK
+PASSES = K // K_PASS
+HALF = 512
+CHUNK = 128
+N_TILES = M // P
+LIST_COLS = 16
+UP_FIRST = 4 * P
+
+SHIFT_ROWS = 112
+
+
+def tile_list_tabgate_silu_kernel(
+    tc, tab_words, tab_scales, w4_words, w4_scales, down, up, gT, b, offs, out
+):
+    nc = tc.nc
+    with ExitStack() as ctx:
+        keep = ctx.enter_context(tc.tile_pool(name="keep", bufs=1))
+        work = ctx.enter_context(tc.tile_pool(name="work", bufs=1))
+        psum = ctx.enter_context(tc.psum_pool(name="psum", bufs=8))
+
+        offsets = keep.tile([P, S // LIST_COLS], U16, name="offsets")
+        nc.sync.dma_start(offsets[:], offs)
+
+        def list_slice(j0, j1):
+            return offsets[:, j0 // LIST_COLS : j1 // LIST_COLS]
+
+        tab_plane = keep.tile([P, T], U8, name="tab_plane", align_bytes=64)
+        nc.vector.memset(tab_plane[:].bitcast(I32), 0)
+        bias_rows = keep.tile([P, P], F32, name="bias_rows")
+        nc.vector.memset(bias_rows[:], 0.0)
+        warm = keep.tile([P, 1], F32, name="warm")
+        nc.vector.memset(warm[:], 0.0)
+        warm_out = keep.tile([P, 1], F32, name="warm_out")
+        nc.scalar.activation(warm_out[:], warm[:], SILU)
+        w4_plane = keep.tile([P, PASSES, M], U8, name="w4_plane", align_bytes=64)
+        nc.vector.memset(w4_plane[:].rearrange("p a n -> p (a n)").bitcast(I32), 0)
+        moved_planes = []
+        for a in range(1, PASSES):
+            plane = keep.tile([P, S], U8, name="moved_plane%d" % a, align_bytes=64)
+            nc.vector.memset(plane[:].bitcast(I32), 0)
+            moved_planes.append(plane)
+        ident = keep.tile([P, P], F32, name="ident")
+        make_identity(nc, ident[:])
+
+        def load_down(a):
+            raw = work.tile([P, PACK, R], F32, name="down_raw%d" % a, tag="eight", bufs=4)
+            nc.sync.dma_start(raw[:], down[a * K_PASS : (a + 1) * K_PASS, :].rearrange("(p j) r -> p j r", j=PACK))
+            return raw
+
+        def load_tab(a):
+            words = keep.tile([P, T], U32, name="tab_words%d" % a, align_bytes=64)
+            nc.sync.dma_start(words[:].bitcast(I32), tab_words[a].rearrange("p t i -> p (t i)").bitcast(I32))
+            return words
+
+        def load_gate(i):
+            gate = keep.tile([P, T], F32, name="gate%d" % i, tag="gate%d" % i, align_bytes=64)
+            nc.sync.dma_start(gate[:], gT[i * P : (i + 1) * P, :])
+            return gate
+
+        def load_up(n0, n1):
+            raw = keep.tile([P, PACK, n1 - n0], F32, name="up_raw%d" % n0)
+            nc.sync.dma_start(raw[:], up[:, n0:n1].rearrange("(p j) n -> p j n", j=PACK))
+            return raw
+
+        def load_w4(n0, n1):
+            words = keep.tile([P, PASSES, 2 * (n1 - n0)], U8, name="w4_words%d" % n0, align_bytes=64)
+            nc.sync.dma_start(
+                words[:].bitcast(I32), w4_words[:, :, 2 * n0 : 2 * n1].rearrange("a p c -> p a c").bitcast(I32)
+            )
+            return words
+
+        tab_win = [load_tab(0)]
+        down_raw = [load_down(0)]
+        for q in range(4):
+            nc.sync.dma_start(
+                tab_plane[32 * q : 32 * q + 4 * PASSES, :].bitcast(I32),
+                tab_scales[:, 4 * q : 4 * q + 4, :].bitcast(I32),
+            )
+        nc.sync.dma_start(bias_rows[0:N_TILES, :], b.rearrange("(i p) -> i p", p=P))
+        down_raw.append(load_down(1))
+        tab_win.append(load_tab(1))
+        down_raw.append(load_down(2))
+        tab_win.append(load_tab(2))
+        up_first = load_up(0, UP_FIRST)
+        for q in range(4):
+            nc.sync.dma_start(
+                w4_plane[32 * q : 32 * q + 4, :, :].bitcast(I32),
+                w4_scales[:, 4 * q : 4 * q + 4, :].rearrange("a r n -> r a n").bitcast(I32),
+            )
+        w4_first = load_w4(0, M // 2)
+        gates = [load_gate(0), load_gate(1)]
+        up_rest = load_up(UP_FIRST, M)
+        gates.append(load_gate(2))
+        w4_second = load_w4(M // 2, M)
+        for i in range(3, N_TILES):
+            gates.append(load_gate(i))
+        w4_halves = [w4_first, w4_second]
+
+        bias_bank = psum.tile([P, HALF], F32, name="bias_bank", tag="bank")
+        nc.tensor.transpose(bias_bank[:, 0:P], bias_rows[:], ident[:])
+        bias = keep.tile([P, N_TILES], F32, name="bias")
+        nc.scalar.copy(bias[:], bias_bank[:, 0:N_TILES])
+
+        picked = [keep.tile([P, S], U32, name="picked%d" % a, align_bytes=64) for a in range(PASSES)]
+
+        def pick_words(a, j0, j1):
+            nc.vector.tensor_copy(picked[a][:, j0:j1], tab_win[a][:].indirect(list_slice(j0, j1)))
+
+        pick_words(0, 0, S)
+        picked_plane = keep.tile([P, S], U8, name="picked_plane", align_bytes=64)
+        nc.vector.tensor_copy(picked_plane[:], tab_plane[:].indirect(offsets[:]))
+        for a in range(1, PASSES):
+            nc.gpsimd.dma_start(
+                moved_planes[a - 1][0:SHIFT_ROWS, :].bitcast(I32),
+                picked_plane[4 * a : 4 * a + SHIFT_ROWS, :].bitcast(I32),
+            )
+        base_planes = [picked_plane] + moved_planes
+
+        down_codes = [keep.tile([P, R], U32, name="down_codes%d" % a, align_bytes=64) for a in range(PASSES)]
+        down_scales = [keep.tile([P, R], U8, name="down_scales%d" % a, align_bytes=64) for a in range(PASSES)]
+        h_banks = [psum.tile([P, PACK, CHUNK], F32, name="h_bank%d" % c, tag="bank") for c in range(S // CHUNK)]
+
+        def h_passes(a, c0, c1):
+            for c in range(c0, c1):
+                cols = slice(c * CHUNK, (c + 1) * CHUNK)
+                for t in range(PACK):
+                    nc.tensor.matmul_mx(
+                        out=h_banks[c][:, t, :],
+                        lhsT=down_codes[a][:, t * P : (t + 1) * P].bitcast(FP8X4),
+                        lhsT_scale=down_scales[a][:, t * P : (t + 1) * P],
+                        rhs=picked[a][:, cols].bitcast(FP8X4),
+                        rhs_scale=picked_plane[4 * a : P, cols],
+                        start=(a == 0 and t == 0),
+                        stop=(a == PASSES - 1 and t == PACK - 1),
+                    )
+
+        for a in range(PASSES):
+            grouped = work.tile([P, PACK, P, PACK], BF16, name="down_bf%d" % a, tag="down_bf", bufs=2, align_bytes=64)
+            dst = grouped[:].rearrange("p t m j -> p m t j")
+            src = down_raw[a][:].rearrange("p j (m t) -> p m t j", t=PACK)
+            if a < PASSES - 1:
+                nc.scalar.copy(dst, src)
+            else:
+                nc.scalar.copy(dst[:, 0 : P // 2], src[:, 0 : P // 2])
+                nc.vector.tensor_copy(dst[:, P // 2 : P], src[:, P // 2 : P])
+            nc.vector.quantize_mx(
+                out=down_codes[a][:].bitcast(FP8X4),
+                scales=down_scales[a][:],
+                in_=grouped[:].rearrange("p t m j -> p (t m j)"),
+            )
+            if a < PASSES - 1:
+                h_passes(a, 0, S // CHUNK)
+            if a == 0:
+                pick_words(1, 0, S)
+
+        h_codes = keep.tile([P, S], U32, name="h_codes", align_bytes=64)
+        h_scales = keep.tile([P, S], U8, name="h_scales", align_bytes=64)
+        h_bf = [keep.tile([P, HALF, PACK], BF16, name="h_bf%d" % u, tag="h_bf%d" % u, align_bytes=64) for u in range(2)]
+        per_half = HALF // CHUNK
+        for u in range(2):
+            pick_words(PASSES - 1, u * HALF, (u + 1) * HALF)
+            h_passes(PASSES - 1, u * per_half, (u + 1) * per_half)
+            for c in range(per_half):
+                copy = nc.scalar.copy if c % 2 == 0 else nc.vector.tensor_copy
+                copy(
+                    h_bf[u][:, c * CHUNK : (c + 1) * CHUNK, :],
+                    h_banks[u * per_half + c][:].rearrange("p t j -> p j t"),
+                )
+
+
+        up_codes = {}
+        up_scales = keep.tile([P, M], U8, name="up_scales", align_bytes=64)
+
+        def quantize_up(i0, i1, tag, codes_tag):
+            n0, n1 = i0 * P, i1 * P
+            if n1 <= UP_FIRST:
+                src = up_first[:, :, n0:n1]
+            else:
+                src = up_rest[:, :, n0 - UP_FIRST : n1 - UP_FIRST]
+            grouped = keep.tile([P, n1 - n0, PACK], BF16, name="up_bf%d" % i0, tag=tag, align_bytes=64)
+            nc.scalar.copy(
+                grouped[:].rearrange("p (c i) j -> p c j i", i=4), src.rearrange("p j (c i) -> p c j i", i=4)
+            )
+            codes = keep.tile([P, n1 - n0], U32, name="up_codes%d" % i0, tag=codes_tag, align_bytes=64)
+            for i in range(i0, i1):
+                up_codes[i] = codes[:, (i - i0) * P : (i - i0 + 1) * P]
+            nc.vector.quantize_mx(
+                out=codes[:].bitcast(FP8X4),
+                scales=up_scales[:, n0:n1],
+                in_=grouped[:].rearrange("p n j -> p (n j)"),
+            )
+
+        def quantize_h(u):
+            cols = slice(u * HALF, (u + 1) * HALF)
+            nc.vector.quantize_mx(
+                out=h_codes[:, cols].bitcast(FP8X4),
+                scales=h_scales[:, cols],
+                in_=h_bf[u][:].rearrange("p n j -> p (n j)"),
+            )
+
+        quantize_h(0)
+        quantize_up(0, 1, "up_bf0", "up_codes0")
+        quantize_h(1)
+        quantize_up(1, 2, "h_bf0", "up_codes1")
+
+        pair = None
+        for i in range(N_TILES):
+            rows = slice(i * P, (i + 1) * P)
+            w4_tile = w4_halves[i // (N_TILES // 2)]
+            byte0 = 2 * P * (i % (N_TILES // 2))
+            act = work.tile([P, S], F32, name="act%d" % i, tag="act", bufs=3)
+            for u in range(2):
+                cols = slice(u * HALF, (u + 1) * HALF)
+                bank = psum.tile([P, HALF], F32, name="y_bank%d_%d" % (i, u), tag="bank")
+                passes = [
+                    (w4_tile[:, a, byte0 : byte0 + 2 * P].bitcast(FP4X4), w4_plane[:, a, rows], picked[a], base_planes[a])
+                    for a in range(PASSES)
+                ]
+                low_rank = [(up_codes[i].bitcast(FP8X4), up_scales[:, rows], h_codes, h_scales)]
+                passes = passes + low_rank if (i, u) == (0, 0) else low_rank + passes
+                for step, (weights, weight_plane, moving, moving_plane) in enumerate(passes):
+                    nc.tensor.matmul_mx(
+                        out=bank[:],
+                        lhsT=weights,
+                        lhsT_scale=weight_plane,
+                        rhs=moving[:, cols].bitcast(FP8X4),
+                        rhs_scale=moving_plane[:, cols],
+                        start=(step == 0),
+                        stop=(step == PASSES),
+                    )
+                nc.scalar.activation(act[:, cols], bank[:], SILU, bias=bias[:, i : i + 1])
+            if i % 2 == 0:
+                pair = work.tile([P, 2, S], F32, name="result%d" % i, tag="eight", bufs=4)
+            result = pair[:, i % 2, :]
+            if 0 < i < N_TILES - 1:
+                nc.vector.tensor_tensor(result, gates[i][:].indirect(offsets[:]), act[:], MULT)
+                nc.sync.dma_start(out[rows, :], result)
+            else:
+                for u in range(2):
+                    cols = slice(u * HALF, (u + 1) * HALF)
+                    nc.vector.tensor_tensor(
+                        result[:, cols], gates[i][:].indirect(list_slice(u * HALF, (u + 1) * HALF)), act[:, cols], MULT
+                    )
+                    nc.sync.dma_start(out[rows, cols], result[:, cols])
+            if i == 0:
+                quantize_up(2, 4, "h_bf1", "up_codes2")
+            if i in (1, 3):
+                quantize_up(i + 3, i + 5, "gate%d" % (i - 1), "gate%d" % i)

@@ -25,7 +25,6 @@ HALF = 512
 CHUNK = 128
 N_TILES = M // P
 LIST_COLS = 16
-UP_FIRST = 4 * P
 
 SHIFT_ROWS = 112
 
@@ -102,20 +101,12 @@ def tile_list_tabgate_silu_kernel(
         tab_win.append(load_tab(1))
         down_raw.append(load_down(2))
         tab_win.append(load_tab(2))
-        up_first = load_up(0, UP_FIRST)
+        up_all = load_up(0, M)
         for q in range(4):
             nc.sync.dma_start(
                 w4_plane[32 * q : 32 * q + 4, :, :].bitcast(I32),
                 w4_scales[:, 4 * q : 4 * q + 4, :].rearrange("a r n -> r a n").bitcast(I32),
             )
-        w4_first = load_w4(0, M // 2)
-        gates = [load_gate(0), load_gate(1)]
-        up_rest = load_up(UP_FIRST, M)
-        gates.append(load_gate(2))
-        w4_second = load_w4(M // 2, M)
-        for i in range(3, N_TILES):
-            gates.append(load_gate(i))
-        w4_halves = [w4_first, w4_second]
 
         bias_bank = psum.tile([P, HALF], F32, name="bias_bank", tag="bank")
         nc.tensor.transpose(bias_bank[:, 0:P], bias_rows[:], ident[:])
@@ -131,11 +122,13 @@ def tile_list_tabgate_silu_kernel(
         picked_plane = keep.tile([P, S], U8, name="picked_plane", align_bytes=64)
         nc.vector.tensor_copy(picked_plane[:], tab_plane[:].indirect(offsets[:]))
         for a in range(1, PASSES):
-            nc.gpsimd.dma_start(
+            nc.sync.dma_start(
                 moved_planes[a - 1][0:SHIFT_ROWS, :].bitcast(I32),
                 picked_plane[4 * a : 4 * a + SHIFT_ROWS, :].bitcast(I32),
             )
         base_planes = [picked_plane] + moved_planes
+        w4_tile = load_w4(0, M)
+        gates = [load_gate(i) for i in range(N_TILES)]
 
         down_codes = [keep.tile([P, R], U32, name="down_codes%d" % a, align_bytes=64) for a in range(PASSES)]
         down_scales = [keep.tile([P, R], U8, name="down_scales%d" % a, align_bytes=64) for a in range(PASSES)]
@@ -194,10 +187,7 @@ def tile_list_tabgate_silu_kernel(
 
         def quantize_up(i0, i1, tag, codes_tag):
             n0, n1 = i0 * P, i1 * P
-            if n1 <= UP_FIRST:
-                src = up_first[:, :, n0:n1]
-            else:
-                src = up_rest[:, :, n0 - UP_FIRST : n1 - UP_FIRST]
+            src = up_all[:, :, n0:n1]
             grouped = keep.tile([P, n1 - n0, PACK], BF16, name="up_bf%d" % i0, tag=tag, align_bytes=64)
             nc.scalar.copy(
                 grouped[:].rearrange("p (c i) j -> p c j i", i=4), src.rearrange("p j (c i) -> p c j i", i=4)
@@ -222,13 +212,13 @@ def tile_list_tabgate_silu_kernel(
         quantize_h(0)
         quantize_up(0, 1, "up_bf0", "up_codes0")
         quantize_h(1)
-        quantize_up(1, 2, "h_bf0", "up_codes1")
 
         pair = None
         for i in range(N_TILES):
             rows = slice(i * P, (i + 1) * P)
-            w4_tile = w4_halves[i // (N_TILES // 2)]
-            byte0 = 2 * P * (i % (N_TILES // 2))
+            byte0 = 2 * P * i
+            if i + 1 < N_TILES:
+                quantize_up(i + 1, i + 2, "up_bf%d" % (i + 1), "up_codes%d" % (i + 1))
             act = work.tile([P, S], F32, name="act%d" % i, tag="act", bufs=3)
             for u in range(2):
                 cols = slice(u * HALF, (u + 1) * HALF)
@@ -238,7 +228,7 @@ def tile_list_tabgate_silu_kernel(
                     for a in range(PASSES)
                 ]
                 low_rank = [(up_codes[i].bitcast(FP8X4), up_scales[:, rows], h_codes, h_scales)]
-                passes = passes + low_rank if (i, u) == (0, 0) else low_rank + passes
+                passes = low_rank + passes
                 for step, (weights, weight_plane, moving, moving_plane) in enumerate(passes):
                     nc.tensor.matmul_mx(
                         out=bank[:],
@@ -253,7 +243,7 @@ def tile_list_tabgate_silu_kernel(
             if i % 2 == 0:
                 pair = work.tile([P, 2, S], F32, name="result%d" % i, tag="eight", bufs=4)
             result = pair[:, i % 2, :]
-            if 0 < i < N_TILES - 1:
+            if i < N_TILES - 1:
                 nc.vector.tensor_tensor(result, gates[i][:].indirect(offsets[:]), act[:], MULT)
                 nc.sync.dma_start(out[rows, :], result)
             else:
@@ -263,7 +253,3 @@ def tile_list_tabgate_silu_kernel(
                         result[:, cols], gates[i][:].indirect(list_slice(u * HALF, (u + 1) * HALF)), act[:, cols], MULT
                     )
                     nc.sync.dma_start(out[rows, cols], result[:, cols])
-            if i == 0:
-                quantize_up(2, 4, "h_bf1", "up_codes2")
-            if i in (1, 3):
-                quantize_up(i + 3, i + 5, "gate%d" % (i - 1), "gate%d" % i)

@@ -27,6 +27,7 @@ N_TILES = M // P
 LIST_COLS = 16
 
 SHIFT_ROWS = 112
+EARLY_TILES = 2
 
 
 def tile_list_tabgate_silu_kernel(
@@ -36,7 +37,7 @@ def tile_list_tabgate_silu_kernel(
     with ExitStack() as ctx:
         keep = ctx.enter_context(tc.tile_pool(name="keep", bufs=1))
         work = ctx.enter_context(tc.tile_pool(name="work", bufs=1))
-        psum = ctx.enter_context(tc.psum_pool(name="psum", bufs=8))
+        psum = ctx.enter_context(tc.psum_pool(name="psum", bufs=1))
 
         offsets = keep.tile([P, S // LIST_COLS], U16, name="offsets")
         nc.sync.dma_start(offsets[:], offs)
@@ -44,7 +45,7 @@ def tile_list_tabgate_silu_kernel(
         def list_slice(j0, j1):
             return offsets[:, j0 // LIST_COLS : j1 // LIST_COLS]
 
-        tab_plane = keep.tile([P, T], U8, name="tab_plane", align_bytes=64)
+        tab_plane = keep.tile([P, T], U8, name="tab_plane", tag="tab_plane", align_bytes=64)
         nc.vector.memset(tab_plane[:].bitcast(I32), 0)
         bias_rows = keep.tile([P, P], F32, name="bias_rows")
         nc.vector.memset(bias_rows[:], 0.0)
@@ -68,7 +69,7 @@ def tile_list_tabgate_silu_kernel(
             return raw
 
         def load_tab(a):
-            words = keep.tile([P, T], U32, name="tab_words%d" % a, align_bytes=64)
+            words = keep.tile([P, T], U32, name="tab_words%d" % a, tag="tab_words%d" % a, align_bytes=64)
             nc.sync.dma_start(words[:].bitcast(I32), tab_words[a].rearrange("p t i -> p (t i)").bitcast(I32))
             return words
 
@@ -101,23 +102,23 @@ def tile_list_tabgate_silu_kernel(
         tab_win.append(load_tab(1))
         down_raw.append(load_down(2))
         tab_win.append(load_tab(2))
-        up_all = load_up(0, M)
         for q in range(4):
             nc.sync.dma_start(
                 w4_plane[32 * q : 32 * q + 4, :, :].bitcast(I32),
                 w4_scales[:, 4 * q : 4 * q + 4, :].rearrange("a r n -> r a n").bitcast(I32),
             )
 
-        bias_bank = psum.tile([P, HALF], F32, name="bias_bank", tag="bank")
+        bias_bank = psum.tile([P, HALF], F32, name="bias_bank", tag="bank7")
         nc.tensor.transpose(bias_bank[:, 0:P], bias_rows[:], ident[:])
         bias = keep.tile([P, N_TILES], F32, name="bias")
         nc.scalar.copy(bias[:], bias_bank[:, 0:N_TILES])
 
-        picked = [keep.tile([P, S], U32, name="picked%d" % a, align_bytes=64) for a in range(PASSES)]
+        picked = {}
 
         def pick_words(a, j0, j1):
             nc.vector.tensor_copy(picked[a][:, j0:j1], tab_win[a][:].indirect(list_slice(j0, j1)))
 
+        picked[0] = keep.tile([P, S], U32, name="picked0", align_bytes=64)
         pick_words(0, 0, S)
         picked_plane = keep.tile([P, S], U8, name="picked_plane", align_bytes=64)
         nc.vector.tensor_copy(picked_plane[:], tab_plane[:].indirect(offsets[:]))
@@ -128,11 +129,12 @@ def tile_list_tabgate_silu_kernel(
             )
         base_planes = [picked_plane] + moved_planes
         w4_tile = load_w4(0, M)
+        up_raw = load_up(0, M)
         gates = [load_gate(i) for i in range(N_TILES)]
 
-        down_codes = [keep.tile([P, R], U32, name="down_codes%d" % a, align_bytes=64) for a in range(PASSES)]
+        down_codes = {}
         down_scales = [keep.tile([P, R], U8, name="down_scales%d" % a, align_bytes=64) for a in range(PASSES)]
-        h_banks = [psum.tile([P, PACK, CHUNK], F32, name="h_bank%d" % c, tag="bank") for c in range(S // CHUNK)]
+        h_banks = [psum.tile([P, PACK, CHUNK], F32, name="h_bank%d" % c, tag="bank%d" % c) for c in range(S // CHUNK)]
 
         def h_passes(a, c0, c1):
             for c in range(c0, c1):
@@ -148,98 +150,117 @@ def tile_list_tabgate_silu_kernel(
                         stop=(a == PASSES - 1 and t == PACK - 1),
                     )
 
-        for a in range(PASSES):
-            grouped = work.tile([P, PACK, P, PACK], BF16, name="down_bf%d" % a, tag="down_bf", bufs=2, align_bytes=64)
-            dst = grouped[:].rearrange("p t m j -> p m t j")
-            src = down_raw[a][:].rearrange("p j (m t) -> p m t j", t=PACK)
-            if a < PASSES - 1:
-                nc.scalar.copy(dst, src)
-            else:
-                nc.scalar.copy(dst[:, 0 : P // 2], src[:, 0 : P // 2])
-                nc.vector.tensor_copy(dst[:, P // 2 : P], src[:, P // 2 : P])
+        def quantize_down(a, t0, t1, copy, tag):
+            grouped = keep.tile([P, t1 - t0, P, PACK], BF16, name="down_bf%d_%d" % (a, t0), tag=tag, align_bytes=64)
+            copy(
+                grouped[:].rearrange("p t m j -> p m t j"),
+                down_raw[a][:].rearrange("p j (m t) -> p m t j", t=PACK)[:, :, t0:t1, :],
+            )
             nc.vector.quantize_mx(
-                out=down_codes[a][:].bitcast(FP8X4),
-                scales=down_scales[a][:],
+                out=down_codes[a][:, t0 * P : t1 * P].bitcast(FP8X4),
+                scales=down_scales[a][:, t0 * P : t1 * P],
                 in_=grouped[:].rearrange("p t m j -> p (t m j)"),
             )
-            if a < PASSES - 1:
-                h_passes(a, 0, S // CHUNK)
-            if a == 0:
-                pick_words(1, 0, S)
 
-        h_codes = keep.tile([P, S], U32, name="h_codes", align_bytes=64)
+        down_codes[0] = keep.tile([P, R], U32, name="down_codes0", tag="tab_plane", align_bytes=64)
+        quantize_down(0, 0, PACK, nc.scalar.copy, "down_bf0")
+        h_passes(0, 0, S // CHUNK)
+        picked[1] = keep.tile([P, S], U32, name="picked1", tag="down_bf0", align_bytes=64)
+        pick_words(1, 0, S)
+        down_codes[1] = keep.tile([P, R], U32, name="down_codes1", tag="tab_words1", align_bytes=64)
+        quantize_down(1, 0, PACK, nc.scalar.copy, "down_bf1")
+        h_passes(1, 0, S // CHUNK)
+        down_codes[2] = keep.tile([P, R], U32, name="down_codes2", align_bytes=64)
+        quantize_down(2, 0, PACK // 2, nc.scalar.copy, "down_bf2")
+        quantize_down(2, PACK // 2, PACK, nc.vector.tensor_copy, "down_bf1")
+        picked[2] = keep.tile([P, S], U32, name="picked2", tag="down_bf1", align_bytes=64)
+        pick_words(2, 0, HALF // 2)
+        pick_words(2, HALF // 2, HALF)
+        pick_words(2, HALF, S)
+
         h_scales = keep.tile([P, S], U8, name="h_scales", align_bytes=64)
         h_bf = [keep.tile([P, HALF, PACK], BF16, name="h_bf%d" % u, tag="h_bf%d" % u, align_bytes=64) for u in range(2)]
         per_half = HALF // CHUNK
         for u in range(2):
-            pick_words(PASSES - 1, u * HALF, (u + 1) * HALF)
             h_passes(PASSES - 1, u * per_half, (u + 1) * per_half)
             for c in range(per_half):
-                copy = nc.scalar.copy if c % 2 == 0 else nc.vector.tensor_copy
+                copy = nc.vector.tensor_copy if (u, c) == (0, per_half - 1) else nc.scalar.copy
                 copy(
                     h_bf[u][:, c * CHUNK : (c + 1) * CHUNK, :],
                     h_banks[u * per_half + c][:].rearrange("p t j -> p j t"),
                 )
 
-
-        up_codes = {}
+        up_codes = keep.tile([P, M], U32, name="up_codes", align_bytes=64)
         up_scales = keep.tile([P, M], U8, name="up_scales", align_bytes=64)
 
-        def quantize_up(i0, i1, tag, codes_tag):
-            n0, n1 = i0 * P, i1 * P
-            src = up_all[:, :, n0:n1]
-            grouped = keep.tile([P, n1 - n0, PACK], BF16, name="up_bf%d" % i0, tag=tag, align_bytes=64)
-            nc.scalar.copy(
-                grouped[:].rearrange("p (c i) j -> p c j i", i=4), src.rearrange("p j (c i) -> p c j i", i=4)
-            )
-            codes = keep.tile([P, n1 - n0], U32, name="up_codes%d" % i0, tag=codes_tag, align_bytes=64)
-            for i in range(i0, i1):
-                up_codes[i] = codes[:, (i - i0) * P : (i - i0 + 1) * P]
-            nc.vector.quantize_mx(
-                out=codes[:].bitcast(FP8X4),
-                scales=up_scales[:, n0:n1],
-                in_=grouped[:].rearrange("p n j -> p (n j)"),
-            )
+        def quantize_up(n0, copy, tag):
+            grouped = keep.tile([P, HALF, PACK], BF16, name="up_bf%d" % n0, tag=tag, align_bytes=64)
+            for c0 in (0, HALF // 2):
+                part = grouped[:, c0 : c0 + HALF // 2, :]
+                cols = slice(n0 + c0, n0 + c0 + HALF // 2)
+                copy(
+                    part.rearrange("p (c i) j -> p c j i", i=4),
+                    up_raw[:, :, cols].rearrange("p j (c i) -> p c j i", i=4),
+                )
+                nc.vector.quantize_mx(
+                    out=up_codes[:, cols].bitcast(FP8X4),
+                    scales=up_scales[:, cols],
+                    in_=part.rearrange("p n j -> p (n j)"),
+                )
 
-        def quantize_h(u):
-            cols = slice(u * HALF, (u + 1) * HALF)
+        h_codes = {}
+
+        def quantize_h(u, tag):
+            h_codes[u] = keep.tile([P, HALF], U32, name="h_codes%d" % u, tag=tag, align_bytes=64)
             nc.vector.quantize_mx(
-                out=h_codes[:, cols].bitcast(FP8X4),
-                scales=h_scales[:, cols],
+                out=h_codes[u][:].bitcast(FP8X4),
+                scales=h_scales[:, u * HALF : (u + 1) * HALF],
                 in_=h_bf[u][:].rearrange("p n j -> p (n j)"),
             )
 
-        quantize_h(0)
-        quantize_up(0, 1, "up_bf0", "up_codes0")
-        quantize_h(1)
+        quantize_h(0, "h_codes0")
+        quantize_h(1, "h_codes1")
+        quantize_up(0, nc.vector.tensor_copy, "h_bf1")
+        quantize_up(HALF, nc.scalar.copy, "h_bf0")
+
+        banks = {}
+
+        def y_pass(i, u, step):
+            rows = slice(i * P, (i + 1) * P)
+            cols = slice(u * HALF, (u + 1) * HALF)
+            if step < PASSES:
+                weights = w4_tile[:, step, 2 * P * i : 2 * P * (i + 1)].bitcast(FP4X4)
+                weight_plane, moving, moving_plane = w4_plane[:, step, rows], picked[step][:, cols], base_planes[step]
+            else:
+                weights = up_codes[:, rows].bitcast(FP8X4)
+                weight_plane, moving, moving_plane = up_scales[:, rows], h_codes[u][:], h_scales
+            first, last = (0, PASSES) if i < EARLY_TILES else (PASSES, PASSES - 1)
+            if step == first:
+                banks[i, u] = psum.tile([P, HALF], F32, name="y_bank%d_%d" % (i, u), tag="bank%d" % ((2 * i + u) % 8))
+            nc.tensor.matmul_mx(
+                out=banks[i, u][:],
+                lhsT=weights,
+                lhsT_scale=weight_plane,
+                rhs=moving.bitcast(FP8X4),
+                rhs_scale=moving_plane[:, cols],
+                start=(step == first),
+                stop=(step == last),
+            )
+
+        for i in range(EARLY_TILES):
+            for u in range(2):
+                for step in range(PASSES):
+                    y_pass(i, u, step)
 
         pair = None
         for i in range(N_TILES):
             rows = slice(i * P, (i + 1) * P)
-            byte0 = 2 * P * i
-            if i + 1 < N_TILES:
-                quantize_up(i + 1, i + 2, "up_bf%d" % (i + 1), "up_codes%d" % (i + 1))
-            act = work.tile([P, S], F32, name="act%d" % i, tag="act", bufs=3)
+            act = work.tile([P, S], F32, name="act%d" % i, tag="act", bufs=4)
             for u in range(2):
                 cols = slice(u * HALF, (u + 1) * HALF)
-                bank = psum.tile([P, HALF], F32, name="y_bank%d_%d" % (i, u), tag="bank")
-                passes = [
-                    (w4_tile[:, a, byte0 : byte0 + 2 * P].bitcast(FP4X4), w4_plane[:, a, rows], picked[a], base_planes[a])
-                    for a in range(PASSES)
-                ]
-                low_rank = [(up_codes[i].bitcast(FP8X4), up_scales[:, rows], h_codes, h_scales)]
-                passes = low_rank + passes
-                for step, (weights, weight_plane, moving, moving_plane) in enumerate(passes):
-                    nc.tensor.matmul_mx(
-                        out=bank[:],
-                        lhsT=weights,
-                        lhsT_scale=weight_plane,
-                        rhs=moving[:, cols].bitcast(FP8X4),
-                        rhs_scale=moving_plane[:, cols],
-                        start=(step == 0),
-                        stop=(step == PASSES),
-                    )
-                nc.scalar.activation(act[:, cols], bank[:], SILU, bias=bias[:, i : i + 1])
+                for step in [PASSES] + ([] if i < EARLY_TILES else list(range(PASSES))):
+                    y_pass(i, u, step)
+                nc.scalar.activation(act[:, cols], banks[i, u][:], SILU, bias=bias[:, i : i + 1])
             if i % 2 == 0:
                 pair = work.tile([P, 2, S], F32, name="result%d" % i, tag="eight", bufs=4)
             result = pair[:, i % 2, :]

@@ -102,10 +102,10 @@ def tile_list_tabgate_silu_kernel(
         tab_win.append(load_tab(1))
         down_raw.append(load_down(2))
         tab_win.append(load_tab(2))
-        for q in range(4):
+        for r in range(4):
             nc.sync.dma_start(
-                w4_plane[32 * q : 32 * q + 4, :, :].bitcast(I32),
-                w4_scales[:, 4 * q : 4 * q + 4, :].rearrange("a r n -> r a n").bitcast(I32),
+                w4_plane[r:P:32, :, :].bitcast(I32),
+                w4_scales[:, r:16:4, :].rearrange("a q n -> q a n").bitcast(I32),
             )
 
         bias_bank = psum.tile([P, HALF], F32, name="bias_bank", tag="bank7")
@@ -264,13 +264,15 @@ def tile_list_tabgate_silu_kernel(
             if i % 2 == 0:
                 pair = work.tile([P, 2, S], F32, name="result%d" % i, tag="eight", bufs=4)
             result = pair[:, i % 2, :]
-            if i < N_TILES - 1:
+            if 0 < i < N_TILES - 1:
                 nc.vector.tensor_tensor(result, gates[i][:].indirect(offsets[:]), act[:], MULT)
-                nc.sync.dma_start(out[rows, :], result)
             else:
                 for u in range(2):
                     cols = slice(u * HALF, (u + 1) * HALF)
                     nc.vector.tensor_tensor(
                         result[:, cols], gates[i][:].indirect(list_slice(u * HALF, (u + 1) * HALF)), act[:, cols], MULT
                     )
-                    nc.sync.dma_start(out[rows, cols], result[:, cols])
+                    if i > 0:
+                        nc.sync.dma_start(out[rows, cols], result[:, cols])
+            if i < N_TILES - 1:
+                nc.sync.dma_start(out[rows, :], result)

@@ -27,6 +27,7 @@ N_TILES = M // P
 LIST_COLS = 16
 
 SHIFT_ROWS = 112
+QUARTER = 256
 EARLY_TILES = 2
 
 
@@ -40,7 +41,6 @@ def tile_list_tabgate_silu_kernel(
         psum = ctx.enter_context(tc.psum_pool(name="psum", bufs=1))
 
         offsets = keep.tile([P, S // LIST_COLS], U16, name="offsets")
-        nc.sync.dma_start(offsets[:], offs)
 
         def list_slice(j0, j1):
             return offsets[:, j0 // LIST_COLS : j1 // LIST_COLS]
@@ -91,6 +91,7 @@ def tile_list_tabgate_silu_kernel(
             return words
 
         tab_win = [load_tab(0)]
+        nc.sync.dma_start(offsets[:], offs)
         down_raw = [load_down(0)]
         for q in range(4):
             nc.sync.dma_start(
@@ -128,8 +129,8 @@ def tile_list_tabgate_silu_kernel(
                 picked_plane[4 * a : 4 * a + SHIFT_ROWS, :].bitcast(I32),
             )
         base_planes = [picked_plane] + moved_planes
-        w4_tile = load_w4(0, M)
         up_raw = load_up(0, M)
+        w4_tile = load_w4(0, M)
         gates = [load_gate(i) for i in range(N_TILES)]
 
         down_codes = {}
@@ -170,7 +171,7 @@ def tile_list_tabgate_silu_kernel(
         down_codes[1] = keep.tile([P, R], U32, name="down_codes1", tag="tab_words1", align_bytes=64)
         quantize_down(1, 0, PACK, nc.scalar.copy, "down_bf1")
         h_passes(1, 0, S // CHUNK)
-        down_codes[2] = keep.tile([P, R], U32, name="down_codes2", align_bytes=64)
+        down_codes[2] = keep.tile([P, R], U32, name="down_codes2", tag="down_codes2", align_bytes=64)
         quantize_down(2, 0, PACK // 2, nc.scalar.copy, "down_bf2")
         quantize_down(2, PACK // 2, PACK, nc.vector.tensor_copy, "down_bf1")
         picked[2] = keep.tile([P, S], U32, name="picked2", tag="down_bf1", align_bytes=64)
@@ -193,11 +194,11 @@ def tile_list_tabgate_silu_kernel(
         up_codes = keep.tile([P, M], U32, name="up_codes", align_bytes=64)
         up_scales = keep.tile([P, M], U8, name="up_scales", align_bytes=64)
 
-        def quantize_up(n0, copy, tag):
-            grouped = keep.tile([P, HALF, PACK], BF16, name="up_bf%d" % n0, tag=tag, align_bytes=64)
-            for c0 in (0, HALF // 2):
-                part = grouped[:, c0 : c0 + HALF // 2, :]
-                cols = slice(n0 + c0, n0 + c0 + HALF // 2)
+        def round_up(n0, n1, copy, tag):
+            grouped = keep.tile([P, n1 - n0, PACK], BF16, name="up_bf%d" % n0, tag=tag, align_bytes=64)
+            for c0 in range(0, n1 - n0, QUARTER):
+                part = grouped[:, c0 : c0 + QUARTER, :]
+                cols = slice(n0 + c0, n0 + c0 + QUARTER)
                 copy(
                     part.rearrange("p (c i) j -> p c j i", i=4),
                     up_raw[:, :, cols].rearrange("p j (c i) -> p c j i", i=4),
@@ -219,9 +220,10 @@ def tile_list_tabgate_silu_kernel(
             )
 
         quantize_h(0, "h_codes0")
-        quantize_h(1, "h_codes1")
-        quantize_up(0, nc.vector.tensor_copy, "h_bf1")
-        quantize_up(HALF, nc.scalar.copy, "h_bf0")
+        round_up(0, QUARTER, nc.vector.tensor_copy, "h_bf0")
+        quantize_h(1, "h_bf0")
+        round_up(QUARTER, HALF, nc.vector.tensor_copy, "h_bf1")
+        round_up(HALF, M, nc.scalar.copy, "down_codes2")
 
         banks = {}
 
@@ -234,7 +236,7 @@ def tile_list_tabgate_silu_kernel(
             else:
                 weights = up_codes[:, rows].bitcast(FP8X4)
                 weight_plane, moving, moving_plane = up_scales[:, rows], h_codes[u][:], h_scales
-            first, last = (0, PASSES) if i < EARLY_TILES else (PASSES, PASSES - 1)
+            first, last = (PASSES, PASSES - 1) if i < EARLY_TILES else (0, PASSES)
             if step == first:
                 banks[i, u] = psum.tile([P, HALF], F32, name="y_bank%d_%d" % (i, u), tag="bank%d" % ((2 * i + u) % 8))
             nc.tensor.matmul_mx(
@@ -247,10 +249,9 @@ def tile_list_tabgate_silu_kernel(
                 stop=(step == last),
             )
 
-        for i in range(EARLY_TILES):
-            for u in range(2):
-                for step in range(PASSES):
-                    y_pass(i, u, step)
+        for u in range(2):
+            for i in range(EARLY_TILES):
+                y_pass(i, u, PASSES)
 
         pair = None
         for i in range(N_TILES):
@@ -258,21 +259,21 @@ def tile_list_tabgate_silu_kernel(
             act = work.tile([P, S], F32, name="act%d" % i, tag="act", bufs=4)
             for u in range(2):
                 cols = slice(u * HALF, (u + 1) * HALF)
-                for step in [PASSES] + ([] if i < EARLY_TILES else list(range(PASSES))):
+                for step in range(PASSES if i < EARLY_TILES else PASSES + 1):
                     y_pass(i, u, step)
                 nc.scalar.activation(act[:, cols], banks[i, u][:], SILU, bias=bias[:, i : i + 1])
             if i % 2 == 0:
                 pair = work.tile([P, 2, S], F32, name="result%d" % i, tag="eight", bufs=4)
             result = pair[:, i % 2, :]
-            if 0 < i < N_TILES - 1:
-                nc.vector.tensor_tensor(result, gates[i][:].indirect(offsets[:]), act[:], MULT)
+            if i == 0:
+                cuts = (0, HALF, S)
+            elif i == N_TILES - 1:
+                cuts = (0, HALF, HALF + HALF // 2, S)
             else:
-                for u in range(2):
-                    cols = slice(u * HALF, (u + 1) * HALF)
-                    nc.vector.tensor_tensor(
-                        result[:, cols], gates[i][:].indirect(list_slice(u * HALF, (u + 1) * HALF)), act[:, cols], MULT
-                    )
-                    if i > 0:
-                        nc.sync.dma_start(out[rows, cols], result[:, cols])
+                cuts = (0, S)
+            for j0, j1 in zip(cuts, cuts[1:]):
+                nc.vector.tensor_tensor(result[:, j0:j1], gates[i][:].indirect(list_slice(j0, j1)), act[:, j0:j1], MULT)
+                if i == N_TILES - 1:
+                    nc.sync.dma_start(out[rows, j0:j1], result[:, j0:j1])
             if i < N_TILES - 1:
                 nc.sync.dma_start(out[rows, :], result)

@@ -49,10 +49,6 @@ def tile_list_tabgate_silu_kernel(
         nc.vector.memset(tab_plane[:].bitcast(I32), 0)
         bias_rows = keep.tile([P, P], F32, name="bias_rows")
         nc.vector.memset(bias_rows[:], 0.0)
-        warm = keep.tile([P, 1], F32, name="warm")
-        nc.vector.memset(warm[:], 0.0)
-        warm_out = keep.tile([P, 1], F32, name="warm_out")
-        nc.scalar.activation(warm_out[:], warm[:], SILU)
         w4_plane = keep.tile([P, PASSES, M], U8, name="w4_plane", align_bytes=64)
         nc.vector.memset(w4_plane[:].rearrange("p a n -> p (a n)").bitcast(I32), 0)
         moved_planes = []

@@ -26,7 +26,6 @@ CHUNK = 128
 N_TILES = M // P
 LIST_COLS = 16
 
-SHIFT_ROWS = 112
 QUARTER = 256
 EARLY_TILES = 2
 
@@ -56,6 +55,10 @@ def tile_list_tabgate_silu_kernel(
             plane = keep.tile([P, S], U8, name="moved_plane%d" % a, align_bytes=64)
             nc.vector.memset(plane[:].bitcast(I32), 0)
             moved_planes.append(plane)
+        warm_in = keep.tile([P, 1], F32, name="warm_in")
+        nc.vector.memset(warm_in[:], 0.0)
+        warm_out = keep.tile([P, 1], F32, name="warm_out")
+        nc.scalar.activation(warm_out[:], warm_in[:], SILU)
         ident = keep.tile([P, P], F32, name="ident")
         make_identity(nc, ident[:])
 
@@ -100,7 +103,7 @@ def tile_list_tabgate_silu_kernel(
         down_raw.append(load_down(2))
         tab_win.append(load_tab(2))
         for r in range(4):
-            nc.sync.dma_start(
+            nc.gpsimd.dma_start(
                 w4_plane[r:P:32, :, :].bitcast(I32),
                 w4_scales[:, r:16:4, :].rearrange("a q n -> q a n").bitcast(I32),
             )
@@ -119,13 +122,18 @@ def tile_list_tabgate_silu_kernel(
         pick_words(0, 0, S)
         picked_plane = keep.tile([P, S], U8, name="picked_plane", align_bytes=64)
         nc.vector.tensor_copy(picked_plane[:], tab_plane[:].indirect(offsets[:]))
-        for a in range(1, PASSES):
-            nc.sync.dma_start(
-                moved_planes[a - 1][0:SHIFT_ROWS, :].bitcast(I32),
-                picked_plane[4 * a : 4 * a + SHIFT_ROWS, :].bitcast(I32),
-            )
+
+        def move_plane(a):
+            for r in range(4):
+                nc.sync.dma_start(
+                    moved_planes[a - 1][r:P:32, :].bitcast(I32),
+                    picked_plane[4 * a + r : P : 32, :].bitcast(I32),
+                )
+
         base_planes = [picked_plane] + moved_planes
+        move_plane(1)
         up_raw = load_up(0, M)
+        move_plane(2)
         w4_tile = load_w4(0, M)
         gates = [load_gate(i) for i in range(N_TILES)]
 

@@ -93,7 +93,8 @@ def tile_list_tabgate_silu_kernel(
         nc.sync.dma_start(offsets[:], offs)
         down_raw = [load_down(0)]
         for q in range(4):
-            nc.sync.dma_start(
+            queue = nc.sync if q < 2 else nc.gpsimd
+            queue.dma_start(
                 tab_plane[32 * q : 32 * q + 4 * PASSES, :].bitcast(I32),
                 tab_scales[:, 4 * q : 4 * q + 4, :].bitcast(I32),
             )

@@ -27,7 +27,7 @@ N_TILES = M // P
 LIST_COLS = 16
 
 QUARTER = 256
-EARLY_TILES = 2
+EARLY_TILES = 4
 
 
 def tile_list_tabgate_silu_kernel(
@@ -82,25 +82,22 @@ def tile_list_tabgate_silu_kernel(
             nc.sync.dma_start(raw[:], up[:, n0:n1].rearrange("(p j) n -> p j n", j=PACK))
             return raw
 
-        def load_w4(n0, n1):
-            words = keep.tile([P, PASSES, 2 * (n1 - n0)], U8, name="w4_words%d" % n0, align_bytes=64)
-            nc.sync.dma_start(
-                words[:].bitcast(I32), w4_words[:, :, 2 * n0 : 2 * n1].rearrange("a p c -> p a c").bitcast(I32)
-            )
-            return words
+        def load_w4(a0, a1):
+            words = keep.tile([P, a1 - a0, 2 * M], U8, name="w4_words%d" % a0, align_bytes=64)
+            nc.sync.dma_start(words[:].bitcast(I32), w4_words[a0:a1].rearrange("a p c -> p a c").bitcast(I32))
+            return [words[:, a, :] for a in range(a1 - a0)]
 
         tab_win = [load_tab(0)]
         nc.sync.dma_start(offsets[:], offs)
         down_raw = [load_down(0)]
         for q in range(4):
-            queue = nc.sync if q < 2 else nc.gpsimd
-            queue.dma_start(
+            nc.sync.dma_start(
                 tab_plane[32 * q : 32 * q + 4 * PASSES, :].bitcast(I32),
                 tab_scales[:, 4 * q : 4 * q + 4, :].bitcast(I32),
             )
         nc.sync.dma_start(bias_rows[0:N_TILES, :], b.rearrange("(i p) -> i p", p=P))
-        down_raw.append(load_down(1))
         tab_win.append(load_tab(1))
+        down_raw.append(load_down(1))
         down_raw.append(load_down(2))
         tab_win.append(load_tab(2))
         for r in range(4):
@@ -132,57 +129,65 @@ def tile_list_tabgate_silu_kernel(
                 )
 
         base_planes = [picked_plane] + moved_planes
+        w4_passes = load_w4(0, 1)
         move_plane(1)
         up_raw = load_up(0, M)
         move_plane(2)
-        w4_tile = load_w4(0, M)
+        w4_passes = w4_passes + load_w4(1, PASSES)
         gates = [load_gate(i) for i in range(N_TILES)]
 
         down_codes = {}
         down_scales = [keep.tile([P, R], U8, name="down_scales%d" % a, align_bytes=64) for a in range(PASSES)]
         h_banks = [psum.tile([P, PACK, CHUNK], F32, name="h_bank%d" % c, tag="bank%d" % c) for c in range(S // CHUNK)]
 
-        def h_passes(a, c0, c1):
+        def h_passes(a, c0, c1, slots=(0, 1, 2, 3)):
             for c in range(c0, c1):
                 cols = slice(c * CHUNK, (c + 1) * CHUNK)
-                for t in range(PACK):
+                for n, t in enumerate(slots):
                     nc.tensor.matmul_mx(
                         out=h_banks[c][:, t, :],
                         lhsT=down_codes[a][:, t * P : (t + 1) * P].bitcast(FP8X4),
                         lhsT_scale=down_scales[a][:, t * P : (t + 1) * P],
                         rhs=picked[a][:, cols].bitcast(FP8X4),
                         rhs_scale=picked_plane[4 * a : P, cols],
-                        start=(a == 0 and t == 0),
-                        stop=(a == PASSES - 1 and t == PACK - 1),
+                        start=(a == 0 and n == 0),
+                        stop=(a == PASSES - 1 and n == PACK - 1),
                     )
 
-        def quantize_down(a, t0, t1, copy, tag):
+        def round_down(a, t0, t1, copy, tag):
             grouped = keep.tile([P, t1 - t0, P, PACK], BF16, name="down_bf%d_%d" % (a, t0), tag=tag, align_bytes=64)
             copy(
                 grouped[:].rearrange("p t m j -> p m t j"),
                 down_raw[a][:].rearrange("p j (m t) -> p m t j", t=PACK)[:, :, t0:t1, :],
             )
+            return grouped
+
+        def quantize_down(a, t0, t1, grouped):
             nc.vector.quantize_mx(
                 out=down_codes[a][:, t0 * P : t1 * P].bitcast(FP8X4),
                 scales=down_scales[a][:, t0 * P : t1 * P],
                 in_=grouped[:].rearrange("p t m j -> p (t m j)"),
             )
 
-        down_codes[0] = keep.tile([P, R], U32, name="down_codes0", tag="tab_plane", align_bytes=64)
-        quantize_down(0, 0, PACK, nc.scalar.copy, "down_bf0")
-        h_passes(0, 0, S // CHUNK)
-        picked[1] = keep.tile([P, S], U32, name="picked1", tag="down_bf0", align_bytes=64)
-        pick_words(1, 0, S)
-        down_codes[1] = keep.tile([P, R], U32, name="down_codes1", tag="tab_words1", align_bytes=64)
-        quantize_down(1, 0, PACK, nc.scalar.copy, "down_bf1")
-        h_passes(1, 0, S // CHUNK)
-        down_codes[2] = keep.tile([P, R], U32, name="down_codes2", tag="down_codes2", align_bytes=64)
-        quantize_down(2, 0, PACK // 2, nc.scalar.copy, "down_bf2")
-        quantize_down(2, PACK // 2, PACK, nc.vector.tensor_copy, "down_bf1")
-        picked[2] = keep.tile([P, S], U32, name="picked2", tag="down_bf1", align_bytes=64)
-        pick_words(2, 0, HALF // 2)
-        pick_words(2, HALF // 2, HALF)
-        pick_words(2, HALF, S)
+        for a in range(PASSES):
+            tag = "tab_plane" if a == 0 else "down_codes%d" % a
+            down_codes[a] = keep.tile([P, R], U32, name="down_codes%d" % a, tag=tag, align_bytes=64)
+            low = round_down(a, 0, 2, nc.scalar.copy, "down_low%d" % a)
+            if a == 0:
+                high = round_down(a, 2, PACK, nc.scalar.copy, "down_high0")
+            else:
+                high = round_down(a, 2, PACK, nc.vector.tensor_copy, "down_high0" if a == 1 else "down_low1")
+            quantize_down(a, 0, 2, low)
+            quantize_down(a, 2, PACK, high)
+            if a < PASSES - 1:
+                h_passes(a, 0, S // CHUNK)
+            if a != 1:
+                later = 1 if a == 0 else 2
+                picked[later] = keep.tile([P, S], U32, name="picked%d" % later, tag="down_low%d" % a, align_bytes=64)
+            if a == 0:
+                pick_words(1, 0, S)
+        for j0 in range(0, S, QUARTER):
+            pick_words(2, j0, j0 + QUARTER)
 
         h_scales = keep.tile([P, S], U8, name="h_scales", align_bytes=64)
         h_bf = [keep.tile([P, HALF, PACK], BF16, name="h_bf%d" % u, tag="h_bf%d" % u, align_bytes=64) for u in range(2)]
@@ -190,7 +195,7 @@ def tile_list_tabgate_silu_kernel(
         for u in range(2):
             h_passes(PASSES - 1, u * per_half, (u + 1) * per_half)
             for c in range(per_half):
-                copy = nc.vector.tensor_copy if (u, c) == (0, per_half - 1) else nc.scalar.copy
+                copy = nc.vector.tensor_copy if u * per_half + c in (3, 5, 7) else nc.scalar.copy
                 copy(
                     h_bf[u][:, c * CHUNK : (c + 1) * CHUNK, :],
                     h_banks[u * per_half + c][:].rearrange("p t j -> p j t"),
@@ -199,20 +204,19 @@ def tile_list_tabgate_silu_kernel(
         up_codes = keep.tile([P, M], U32, name="up_codes", align_bytes=64)
         up_scales = keep.tile([P, M], U8, name="up_scales", align_bytes=64)
 
-        def round_up(n0, n1, copy, tag):
-            grouped = keep.tile([P, n1 - n0, PACK], BF16, name="up_bf%d" % n0, tag=tag, align_bytes=64)
-            for c0 in range(0, n1 - n0, QUARTER):
-                part = grouped[:, c0 : c0 + QUARTER, :]
-                cols = slice(n0 + c0, n0 + c0 + QUARTER)
-                copy(
-                    part.rearrange("p (c i) j -> p c j i", i=4),
-                    up_raw[:, :, cols].rearrange("p j (c i) -> p c j i", i=4),
-                )
-                nc.vector.quantize_mx(
-                    out=up_codes[:, cols].bitcast(FP8X4),
-                    scales=up_scales[:, cols],
-                    in_=part.rearrange("p n j -> p (n j)"),
-                )
+        def round_up(n0, copy, grouped):
+            copy(
+                grouped.rearrange("p (c i) j -> p c j i", i=4),
+                up_raw[:, :, n0 : n0 + QUARTER].rearrange("p j (c i) -> p c j i", i=4),
+            )
+            return grouped
+
+        def quantize_up(n0, grouped):
+            nc.vector.quantize_mx(
+                out=up_codes[:, n0 : n0 + QUARTER].bitcast(FP8X4),
+                scales=up_scales[:, n0 : n0 + QUARTER],
+                in_=grouped.rearrange("p n j -> p (n j)"),
+            )
 
         h_codes = {}
 
@@ -225,10 +229,18 @@ def tile_list_tabgate_silu_kernel(
             )
 
         quantize_h(0, "h_codes0")
-        round_up(0, QUARTER, nc.vector.tensor_copy, "h_bf0")
-        quantize_h(1, "h_bf0")
-        round_up(QUARTER, HALF, nc.vector.tensor_copy, "h_bf1")
-        round_up(HALF, M, nc.scalar.copy, "down_codes2")
+        up_early = keep.tile([P, QUARTER, PACK], BF16, name="up_early", tag="h_bf0", align_bytes=64)
+        up_scalar = keep.tile([P, HALF, PACK], BF16, name="up_scalar", tag="down_codes2", align_bytes=64)
+        up_bf0 = round_up(0, nc.vector.tensor_copy, up_early[:])
+        up_bf2 = round_up(2 * QUARTER, nc.scalar.copy, up_scalar[:, 0:QUARTER, :])
+        quantize_h(1, "h_codes1")
+        quantize_up(0, up_bf0)
+        up_late = keep.tile([P, QUARTER, PACK], BF16, name="up_late", tag="h_bf1", align_bytes=64)
+        up_bf1 = round_up(QUARTER, nc.vector.tensor_copy, up_late[:])
+        up_bf3 = round_up(3 * QUARTER, nc.scalar.copy, up_scalar[:, QUARTER:HALF, :])
+        quantize_up(2 * QUARTER, up_bf2)
+        quantize_up(QUARTER, up_bf1)
+        quantize_up(3 * QUARTER, up_bf3)
 
         banks = {}
 
@@ -236,14 +248,14 @@ def tile_list_tabgate_silu_kernel(
             rows = slice(i * P, (i + 1) * P)
             cols = slice(u * HALF, (u + 1) * HALF)
             if step < PASSES:
-                weights = w4_tile[:, step, 2 * P * i : 2 * P * (i + 1)].bitcast(FP4X4)
+                weights = w4_passes[step][:, 2 * P * i : 2 * P * (i + 1)].bitcast(FP4X4)
                 weight_plane, moving, moving_plane = w4_plane[:, step, rows], picked[step][:, cols], base_planes[step]
             else:
                 weights = up_codes[:, rows].bitcast(FP8X4)
                 weight_plane, moving, moving_plane = up_scales[:, rows], h_codes[u][:], h_scales
-            first, last = (PASSES, PASSES - 1) if i < EARLY_TILES else (0, PASSES)
+            first, last = 0, PASSES
             if step == first:
-                banks[i, u] = psum.tile([P, HALF], F32, name="y_bank%d_%d" % (i, u), tag="bank%d" % ((2 * i + u) % 8))
+                banks[i, u] = psum.tile([P, HALF], F32, name="y_bank%d_%d" % (i, u), tag="bank%d" % (5 + (2 * i + u) % 3))
             nc.tensor.matmul_mx(
                 out=banks[i, u][:],
                 lhsT=weights,
@@ -254,9 +266,6 @@ def tile_list_tabgate_silu_kernel(
                 stop=(step == last),
             )
 
-        for u in range(2):
-            for i in range(EARLY_TILES):
-                y_pass(i, u, PASSES)
 
         pair = None
         for i in range(N_TILES):
@@ -264,7 +273,7 @@ def tile_list_tabgate_silu_kernel(
             act = work.tile([P, S], F32, name="act%d" % i, tag="act", bufs=4)
             for u in range(2):
                 cols = slice(u * HALF, (u + 1) * HALF)
-                for step in range(PASSES if i < EARLY_TILES else PASSES + 1):
+                for step in range(PASSES + 1):
                     y_pass(i, u, step)
                 nc.scalar.activation(act[:, cols], banks[i, u][:], SILU, bias=bias[:, i : i + 1])
             if i % 2 == 0:

@@ -55,10 +55,6 @@ def tile_list_tabgate_silu_kernel(
             plane = keep.tile([P, S], U8, name="moved_plane%d" % a, align_bytes=64)
             nc.vector.memset(plane[:].bitcast(I32), 0)
             moved_planes.append(plane)
-        warm_in = keep.tile([P, 1], F32, name="warm_in")
-        nc.vector.memset(warm_in[:], 0.0)
-        warm_out = keep.tile([P, 1], F32, name="warm_out")
-        nc.scalar.activation(warm_out[:], warm_in[:], SILU)
         ident = keep.tile([P, P], F32, name="ident")
         make_identity(nc, ident[:])
 

@@ -21,13 +21,14 @@ P = 128
 PACK = 4
 K_PASS = P * PACK
 PASSES = K // K_PASS
+SCALE_ROWS = 16
 HALF = 512
+QUARTER = 256
 CHUNK = 128
 N_TILES = M // P
 LIST_COLS = 16
-
-QUARTER = 256
-EARLY_TILES = 4
+ROW0 = 36
+Y_BANKS = 2
 
 
 def tile_list_tabgate_silu_kernel(
@@ -41,249 +42,233 @@ def tile_list_tabgate_silu_kernel(
 
         offsets = keep.tile([P, S // LIST_COLS], U16, name="offsets")
 
-        def list_slice(j0, j1):
+        def entries(j0, j1):
             return offsets[:, j0 // LIST_COLS : j1 // LIST_COLS]
 
-        tab_plane = keep.tile([P, T], U8, name="tab_plane", tag="tab_plane", align_bytes=64)
-        nc.vector.memset(tab_plane[:].bitcast(I32), 0)
+        scale_window = keep.tile([P, T], U8, name="scale_window", tag="scale_window", align_bytes=64)
+        nc.vector.memset(scale_window[:].bitcast(I32), 0)
+        tab_planes = keep.tile([P, PASSES, S], U8, name="tab_planes", align_bytes=64)
+        nc.vector.memset(tab_planes[:].rearrange("p a n -> p (a n)").bitcast(I32), 0)
+        w4_planes = keep.tile([P, PASSES, M], U8, name="w4_planes", align_bytes=64)
+        nc.vector.memset(w4_planes[:].rearrange("p a n -> p (a n)").bitcast(I32), 0)
         bias_rows = keep.tile([P, P], F32, name="bias_rows")
-        nc.vector.memset(bias_rows[:], 0.0)
-        w4_plane = keep.tile([P, PASSES, M], U8, name="w4_plane", align_bytes=64)
-        nc.vector.memset(w4_plane[:].rearrange("p a n -> p (a n)").bitcast(I32), 0)
-        moved_planes = []
-        for a in range(1, PASSES):
-            plane = keep.tile([P, S], U8, name="moved_plane%d" % a, align_bytes=64)
-            nc.vector.memset(plane[:].bitcast(I32), 0)
-            moved_planes.append(plane)
+        nc.gpsimd.memset(bias_rows[:], 0.0)
         ident = keep.tile([P, P], F32, name="ident")
         make_identity(nc, ident[:])
+        warm = keep.tile([P, 1], F32, name="warm")
+        nc.scalar.activation(warm[:], ident[:, 0:1], SILU)
+        nc.gpsimd.dma_start(bias_rows[0:N_TILES, :], b.rearrange("(i p) -> i p", p=P))
+        for r in range(PACK):
+            nc.gpsimd.dma_start(
+                w4_planes[r:P:32, :, :].bitcast(I32),
+                w4_scales[:, r:SCALE_ROWS:PACK, :].rearrange("a q n -> q a n").bitcast(I32),
+            )
 
-        def load_down(a):
-            raw = work.tile([P, PACK, R], F32, name="down_raw%d" % a, tag="eight", bufs=4)
-            nc.sync.dma_start(raw[:], down[a * K_PASS : (a + 1) * K_PASS, :].rearrange("(p j) r -> p j r", j=PACK))
-            return raw
-
-        def load_tab(a):
-            words = keep.tile([P, T], U32, name="tab_words%d" % a, tag="tab_words%d" % a, align_bytes=64)
+        def load_tab(a, tag):
+            words = keep.tile([P, T], U32, name="tab_words%d" % a, tag=tag, align_bytes=64)
             nc.sync.dma_start(words[:].bitcast(I32), tab_words[a].rearrange("p t i -> p (t i)").bitcast(I32))
             return words
 
-        def load_gate(i):
-            gate = keep.tile([P, T], F32, name="gate%d" % i, tag="gate%d" % i, align_bytes=64)
-            nc.sync.dma_start(gate[:], gT[i * P : (i + 1) * P, :])
-            return gate
-
-        def load_up(n0, n1):
-            raw = keep.tile([P, PACK, n1 - n0], F32, name="up_raw%d" % n0)
-            nc.sync.dma_start(raw[:], up[:, n0:n1].rearrange("(p j) n -> p j n", j=PACK))
+        def load_down(a, tag):
+            raw = keep.tile([P, PACK, R], F32, name="down_raw%d" % a, tag=tag, align_bytes=64)
+            nc.sync.dma_start(raw[:], down[a * K_PASS : (a + 1) * K_PASS, :].rearrange("(p j) r -> p j r", j=PACK))
             return raw
 
-        def load_w4(a0, a1):
-            words = keep.tile([P, a1 - a0, 2 * M], U8, name="w4_words%d" % a0, align_bytes=64)
+        def load_w4(a0, a1, tag):
+            words = keep.tile([P, a1 - a0, 2 * M], U8, name="w4_words%d" % a0, tag=tag, align_bytes=64)
             nc.sync.dma_start(words[:].bitcast(I32), w4_words[a0:a1].rearrange("a p c -> p a c").bitcast(I32))
             return [words[:, a, :] for a in range(a1 - a0)]
 
-        tab_win = [load_tab(0)]
+        def load_gate(i, tag):
+            gate = keep.tile([P, T], F32, name="gate%d" % i, tag=tag, align_bytes=64)
+            nc.sync.dma_start(gate[:], gT[i * P : (i + 1) * P, :])
+            return gate
+
+        tab_win = [load_tab(0, "tab0")]
         nc.sync.dma_start(offsets[:], offs)
-        down_raw = [load_down(0)]
-        for q in range(4):
+        for a in range(PASSES):
+            first = ROW0 + 4 * a
             nc.sync.dma_start(
-                tab_plane[32 * q : 32 * q + 4 * PASSES, :].bitcast(I32),
-                tab_scales[:, 4 * q : 4 * q + 4, :].bitcast(I32),
+                scale_window[first : first + 3 * (SCALE_ROWS - 1) + 1 : 3, :].bitcast(I32),
+                tab_scales[a].bitcast(I32),
             )
-        nc.sync.dma_start(bias_rows[0:N_TILES, :], b.rearrange("(i p) -> i p", p=P))
-        tab_win.append(load_tab(1))
-        down_raw.append(load_down(1))
-        down_raw.append(load_down(2))
-        tab_win.append(load_tab(2))
-        for r in range(4):
-            nc.gpsimd.dma_start(
-                w4_plane[r:P:32, :, :].bitcast(I32),
-                w4_scales[:, r:16:4, :].rearrange("a q n -> q a n").bitcast(I32),
+        down_raw = [load_down(0, "down0")]
+        tab_win.append(load_tab(1, "tab1"))
+        down_raw.append(load_down(1, "down1"))
+        w4_passes = load_w4(0, 1, "w4_first")
+
+        picked_rows = keep.tile([P, S], U8, name="picked_rows", tag="picked_rows", align_bytes=64)
+        nc.vector.tensor_copy(picked_rows[:], scale_window[:].indirect(offsets[:]))
+        for r in range(PACK):
+            first = ROW0 + 3 * r
+            nc.sync.dma_start(
+                tab_planes[r:P:32, :, :].rearrange("p a n -> p (a n)").bitcast(I32),
+                picked_rows[first : first + 4 * (4 * PASSES - 1) + 1 : 4, :].bitcast(I32),
             )
 
-        bias_bank = psum.tile([P, HALF], F32, name="bias_bank", tag="bank7")
-        nc.tensor.transpose(bias_bank[:, 0:P], bias_rows[:], ident[:])
-        bias = keep.tile([P, N_TILES], F32, name="bias")
-        nc.scalar.copy(bias[:], bias_bank[:, 0:N_TILES])
-
-        picked = {}
-
-        def pick_words(a, j0, j1):
-            nc.vector.tensor_copy(picked[a][:, j0:j1], tab_win[a][:].indirect(list_slice(j0, j1)))
-
-        picked[0] = keep.tile([P, S], U32, name="picked0", align_bytes=64)
-        pick_words(0, 0, S)
-        picked_plane = keep.tile([P, S], U8, name="picked_plane", align_bytes=64)
-        nc.vector.tensor_copy(picked_plane[:], tab_plane[:].indirect(offsets[:]))
-
-        def move_plane(a):
-            for r in range(4):
-                nc.sync.dma_start(
-                    moved_planes[a - 1][r:P:32, :].bitcast(I32),
-                    picked_plane[4 * a + r : P : 32, :].bitcast(I32),
-                )
-
-        base_planes = [picked_plane] + moved_planes
-        w4_passes = load_w4(0, 1)
-        move_plane(1)
-        up_raw = load_up(0, M)
-        move_plane(2)
-        w4_passes = w4_passes + load_w4(1, PASSES)
-        gates = [load_gate(i) for i in range(N_TILES)]
-
-        down_codes = {}
-        down_scales = [keep.tile([P, R], U8, name="down_scales%d" % a, align_bytes=64) for a in range(PASSES)]
+        picked = [
+            keep.tile([P, S], U32, name="picked%d" % a, tag="scale_window" if a == 0 else "picked%d" % a, align_bytes=64)
+            for a in range(PASSES)
+        ]
+        down_codes = [keep.tile([P, R], U32, name="down_codes%d" % a, tag="down_codes%d" % a, align_bytes=64) for a in range(PASSES)]
+        down_scales = [keep.tile([P, R], U8, name="down_scales%d" % a, tag="down_scales%d" % a, align_bytes=64) for a in range(PASSES)]
         h_banks = [psum.tile([P, PACK, CHUNK], F32, name="h_bank%d" % c, tag="bank%d" % c) for c in range(S // CHUNK)]
 
-        def h_passes(a, c0, c1, slots=(0, 1, 2, 3)):
+        def pick_words(a, j0, j1):
+            nc.vector.tensor_copy(picked[a][:, j0:j1], tab_win[a][:].indirect(entries(j0, j1)))
+
+        def round_down(a, t0, copy):
+            grouped = keep.tile([P, 2, P, PACK], BF16, name="down_bf%d_%d" % (a, t0), tag="down_bf%d_%d" % (a, t0), align_bytes=64)
+            copy(
+                grouped[:].rearrange("p t m j -> p m t j"),
+                down_raw[a][:].rearrange("p j (m t) -> p m t j", t=PACK)[:, :, t0 : t0 + 2, :],
+            )
+            return grouped
+
+        def quantize_down(a, t0, grouped):
+            nc.vector.quantize_mx(
+                out=down_codes[a][:, t0 * P : (t0 + 2) * P].bitcast(FP8X4),
+                scales=down_scales[a][:, t0 * P : (t0 + 2) * P],
+                in_=grouped[:].rearrange("p t m j -> p (t m j)"),
+            )
+
+        def h_passes(a, c0, c1):
             for c in range(c0, c1):
                 cols = slice(c * CHUNK, (c + 1) * CHUNK)
-                for n, t in enumerate(slots):
+                for t in range(PACK):
                     nc.tensor.matmul_mx(
                         out=h_banks[c][:, t, :],
                         lhsT=down_codes[a][:, t * P : (t + 1) * P].bitcast(FP8X4),
                         lhsT_scale=down_scales[a][:, t * P : (t + 1) * P],
                         rhs=picked[a][:, cols].bitcast(FP8X4),
-                        rhs_scale=picked_plane[4 * a : P, cols],
-                        start=(a == 0 and n == 0),
-                        stop=(a == PASSES - 1 and n == PACK - 1),
+                        rhs_scale=tab_planes[:, a, cols],
+                        start=(a == 0 and t == 0),
+                        stop=(a == PASSES - 1 and t == PACK - 1),
                     )
 
-        def round_down(a, t0, t1, copy, tag):
-            grouped = keep.tile([P, t1 - t0, P, PACK], BF16, name="down_bf%d_%d" % (a, t0), tag=tag, align_bytes=64)
-            copy(
-                grouped[:].rearrange("p t m j -> p m t j"),
-                down_raw[a][:].rearrange("p j (m t) -> p m t j", t=PACK)[:, :, t0:t1, :],
-            )
-            return grouped
+        def prepare_down(a, second_copy):
+            low = round_down(a, 0, nc.scalar.copy)
+            high = round_down(a, 2, second_copy)
+            quantize_down(a, 0, low)
+            quantize_down(a, 2, high)
 
-        def quantize_down(a, t0, t1, grouped):
-            nc.vector.quantize_mx(
-                out=down_codes[a][:, t0 * P : t1 * P].bitcast(FP8X4),
-                scales=down_scales[a][:, t0 * P : t1 * P],
-                in_=grouped[:].rearrange("p t m j -> p (t m j)"),
-            )
-
-        for a in range(PASSES):
-            tag = "tab_plane" if a == 0 else "down_codes%d" % a
-            down_codes[a] = keep.tile([P, R], U32, name="down_codes%d" % a, tag=tag, align_bytes=64)
-            low = round_down(a, 0, 2, nc.scalar.copy, "down_low%d" % a)
-            if a == 0:
-                high = round_down(a, 2, PACK, nc.scalar.copy, "down_high0")
-            else:
-                high = round_down(a, 2, PACK, nc.vector.tensor_copy, "down_high0" if a == 1 else "down_low1")
-            quantize_down(a, 0, 2, low)
-            quantize_down(a, 2, PACK, high)
-            if a < PASSES - 1:
-                h_passes(a, 0, S // CHUNK)
-            if a != 1:
-                later = 1 if a == 0 else 2
-                picked[later] = keep.tile([P, S], U32, name="picked%d" % later, tag="down_low%d" % a, align_bytes=64)
-            if a == 0:
-                pick_words(1, 0, S)
-        for j0 in range(0, S, QUARTER):
-            pick_words(2, j0, j0 + QUARTER)
-
-        h_scales = keep.tile([P, S], U8, name="h_scales", align_bytes=64)
-        h_bf = [keep.tile([P, HALF, PACK], BF16, name="h_bf%d" % u, tag="h_bf%d" % u, align_bytes=64) for u in range(2)]
+        pick_words(0, 0, S)
+        down_raw.append(load_down(2, "tab0"))
+        prepare_down(0, nc.scalar.copy)
+        tab_win.append(load_tab(2, "down0"))
+        up_raw = keep.tile([P, PACK, M], F32, name="up_raw", tag="down_bf0_0", align_bytes=64)
+        nc.sync.dma_start(up_raw[:], up.rearrange("(p j) n -> p j n", j=PACK))
         per_half = HALF // CHUNK
+        h_passes(0, 0, 2 * per_half)
+        w4_passes = w4_passes + load_w4(1, PASSES, "down_bf0_2")
+        pick_words(1, 0, S)
+        prepare_down(1, nc.vector.tensor_copy)
+        gates = [load_gate(0, "down1"), load_gate(1, "down_bf1_0"), load_gate(2, "down_bf1_2")]
+        h_passes(1, 0, 2 * per_half)
+        prepare_down(2, nc.vector.tensor_copy)
+        gates = gates + [load_gate(3, "tab0"), load_gate(4, "down_bf2_0"), load_gate(5, "down_bf2_2")]
+        for j0 in range(0, S, QUARTER):
+            pick_words(PASSES - 1, j0, j0 + QUARTER)
+        gates.append(load_gate(6, "down0"))
+
+        h_bf = [keep.tile([P, HALF, PACK], BF16, name="h_bf%d" % u, tag="h_bf%d" % u, align_bytes=64) for u in range(2)]
+        h_codes = {}
+        h_scales = [keep.tile([P, HALF], U8, name="h_scales%d" % u, align_bytes=64) for u in range(2)]
         for u in range(2):
             h_passes(PASSES - 1, u * per_half, (u + 1) * per_half)
             for c in range(per_half):
-                copy = nc.vector.tensor_copy if u * per_half + c in (3, 5, 7) else nc.scalar.copy
+                copy = nc.vector.tensor_copy if u * per_half + c in (3, 5) else nc.scalar.copy
                 copy(
                     h_bf[u][:, c * CHUNK : (c + 1) * CHUNK, :],
                     h_banks[u * per_half + c][:].rearrange("p t j -> p j t"),
                 )
+        bias_bank = psum.tile([P, HALF], F32, name="bias_bank", tag="bank0")
+        nc.tensor.transpose(bias_bank[:, 0:P], bias_rows[:], ident[:])
+        bias_cols = []
+        for i0, i1 in ((0, 1), (1, N_TILES)):
+            part = keep.tile([P, i1 - i0], F32, name="bias%d" % i0, tag="bias%d" % i0, align_bytes=64)
+            nc.scalar.copy(part[:], bias_bank[:, i0:i1])
+            bias_cols = bias_cols + [part[:, i : i + 1] for i in range(i1 - i0)]
 
-        up_codes = keep.tile([P, M], U32, name="up_codes", align_bytes=64)
-        up_scales = keep.tile([P, M], U8, name="up_scales", align_bytes=64)
-
-        def round_up(n0, copy, grouped):
-            copy(
-                grouped.rearrange("p (c i) j -> p c j i", i=4),
-                up_raw[:, :, n0 : n0 + QUARTER].rearrange("p j (c i) -> p c j i", i=4),
-            )
-            return grouped
-
-        def quantize_up(n0, grouped):
-            nc.vector.quantize_mx(
-                out=up_codes[:, n0 : n0 + QUARTER].bitcast(FP8X4),
-                scales=up_scales[:, n0 : n0 + QUARTER],
-                in_=grouped.rearrange("p n j -> p (n j)"),
-            )
-
-        h_codes = {}
 
         def quantize_h(u, tag):
             h_codes[u] = keep.tile([P, HALF], U32, name="h_codes%d" % u, tag=tag, align_bytes=64)
             nc.vector.quantize_mx(
                 out=h_codes[u][:].bitcast(FP8X4),
-                scales=h_scales[:, u * HALF : (u + 1) * HALF],
+                scales=h_scales[u][:],
                 in_=h_bf[u][:].rearrange("p n j -> p (n j)"),
             )
 
-        quantize_h(0, "h_codes0")
-        up_early = keep.tile([P, QUARTER, PACK], BF16, name="up_early", tag="h_bf0", align_bytes=64)
-        up_scalar = keep.tile([P, HALF, PACK], BF16, name="up_scalar", tag="down_codes2", align_bytes=64)
-        up_bf0 = round_up(0, nc.vector.tensor_copy, up_early[:])
-        up_bf2 = round_up(2 * QUARTER, nc.scalar.copy, up_scalar[:, 0:QUARTER, :])
-        quantize_h(1, "h_codes1")
-        quantize_up(0, up_bf0)
-        up_late = keep.tile([P, QUARTER, PACK], BF16, name="up_late", tag="h_bf1", align_bytes=64)
-        up_bf1 = round_up(QUARTER, nc.vector.tensor_copy, up_late[:])
-        up_bf3 = round_up(3 * QUARTER, nc.scalar.copy, up_scalar[:, QUARTER:HALF, :])
-        quantize_up(2 * QUARTER, up_bf2)
-        quantize_up(QUARTER, up_bf1)
-        quantize_up(3 * QUARTER, up_bf3)
+        up_codes = {}
+        up_scales = keep.tile([P, M], U8, name="up_scales", align_bytes=64)
 
-        banks = {}
+        def round_up(q, copy, tag):
+            cols = slice(q * QUARTER, (q + 1) * QUARTER)
+            grouped = keep.tile([P, QUARTER, PACK], BF16, name="up_bf%d" % q, tag=tag, align_bytes=64)
+            copy(
+                grouped[:].rearrange("p (c i) j -> p c j i", i=4),
+                up_raw[:, :, cols].rearrange("p j (c i) -> p c j i", i=4),
+            )
+            return grouped
 
-        def y_pass(i, u, step):
-            rows = slice(i * P, (i + 1) * P)
-            cols = slice(u * HALF, (u + 1) * HALF)
-            if step < PASSES:
-                weights = w4_passes[step][:, 2 * P * i : 2 * P * (i + 1)].bitcast(FP4X4)
-                weight_plane, moving, moving_plane = w4_plane[:, step, rows], picked[step][:, cols], base_planes[step]
-            else:
-                weights = up_codes[:, rows].bitcast(FP8X4)
-                weight_plane, moving, moving_plane = up_scales[:, rows], h_codes[u][:], h_scales
-            first, last = 0, PASSES
-            if step == first:
-                banks[i, u] = psum.tile([P, HALF], F32, name="y_bank%d_%d" % (i, u), tag="bank%d" % (5 + (2 * i + u) % 3))
-            nc.tensor.matmul_mx(
-                out=banks[i, u][:],
-                lhsT=weights,
-                lhsT_scale=weight_plane,
-                rhs=moving.bitcast(FP8X4),
-                rhs_scale=moving_plane[:, cols],
-                start=(step == first),
-                stop=(step == last),
+        def quantize_up(q, grouped, tag):
+            up_codes[q] = keep.tile([P, QUARTER], U32, name="up_codes%d" % q, tag=tag, align_bytes=64)
+            nc.vector.quantize_mx(
+                out=up_codes[q][:].bitcast(FP8X4),
+                scales=up_scales[:, q * QUARTER : (q + 1) * QUARTER],
+                in_=grouped[:].rearrange("p n j -> p (n j)"),
             )
 
+        quantize_h(0, "h_codes0")
+        quantize_up(0, round_up(0, nc.vector.tensor_copy, "h_bf0"), "up_codes0")
+        quantize_h(1, "h_bf0")
+        quantize_up(1, round_up(1, nc.vector.tensor_copy, "h_bf1"), "up_codes1")
+        quantize_up(2, round_up(2, nc.scalar.copy, "down_codes2"), "up_codes2")
+        gates.append(load_gate(7, "h_bf1"))
 
-        pair = None
         for i in range(N_TILES):
             rows = slice(i * P, (i + 1) * P)
             act = work.tile([P, S], F32, name="act%d" % i, tag="act", bufs=4)
             for u in range(2):
                 cols = slice(u * HALF, (u + 1) * HALF)
-                for step in range(PASSES + 1):
-                    y_pass(i, u, step)
-                nc.scalar.activation(act[:, cols], banks[i, u][:], SILU, bias=bias[:, i : i + 1])
-            if i % 2 == 0:
-                pair = work.tile([P, 2, S], F32, name="result%d" % i, tag="eight", bufs=4)
-            result = pair[:, i % 2, :]
+                bank = psum.tile(
+                    [P, HALF], F32, name="y_bank%d_%d" % (i, u), tag="bank%d" % (4 + (2 * i + u) % Y_BANKS)
+                )
+                for a in range(PASSES):
+                    nc.tensor.matmul_mx(
+                        out=bank[:],
+                        lhsT=w4_passes[a][:, 2 * P * i : 2 * P * (i + 1)].bitcast(FP4X4),
+                        lhsT_scale=w4_planes[:, a, rows],
+                        rhs=picked[a][:, cols].bitcast(FP8X4),
+                        rhs_scale=tab_planes[:, a, cols],
+                        start=(a == 0),
+                        stop=False,
+                    )
+                nc.tensor.matmul_mx(
+                    out=bank[:],
+                    lhsT=up_codes[i // 2][:, (i % 2) * P : (i % 2 + 1) * P].bitcast(FP8X4),
+                    lhsT_scale=up_scales[:, rows],
+                    rhs=h_codes[u][:].bitcast(FP8X4),
+                    rhs_scale=h_scales[u][:],
+                    start=False,
+                    stop=True,
+                )
+                nc.scalar.activation(act[:, cols], bank[:], SILU, bias=bias_cols[i])
+            if i == 0:
+                late_up = round_up(3, nc.scalar.copy, "bias0")
+            tag = "bias0" if i == 3 else "result%d" % i
+            result = keep.tile([P, S], F32, name="result%d" % i, tag=tag, align_bytes=64)
             if i == 0:
                 cuts = (0, HALF, S)
             elif i == N_TILES - 1:
-                cuts = (0, HALF, HALF + HALF // 2, S)
+                cuts = (0, HALF, HALF + QUARTER, S)
             else:
                 cuts = (0, S)
             for j0, j1 in zip(cuts, cuts[1:]):
-                nc.vector.tensor_tensor(result[:, j0:j1], gates[i][:].indirect(list_slice(j0, j1)), act[:, j0:j1], MULT)
+                nc.vector.tensor_tensor(result[:, j0:j1], gates[i][:].indirect(entries(j0, j1)), act[:, j0:j1], MULT)
                 if i == N_TILES - 1:
                     nc.sync.dma_start(out[rows, j0:j1], result[:, j0:j1])
             if i < N_TILES - 1:
-                nc.sync.dma_start(out[rows, :], result)
+                nc.sync.dma_start(out[rows, :], result[:])
+            if i == 1:
+                quantize_up(3, late_up, "down_bf1_0")

@@ -27,8 +27,7 @@ QUARTER = 256
 CHUNK = 128
 N_TILES = M // P
 LIST_COLS = 16
-ROW0 = 36
-Y_BANKS = 2
+Y_BANKS = 3
 
 
 def tile_list_tabgate_silu_kernel(
@@ -47,8 +46,8 @@ def tile_list_tabgate_silu_kernel(
 
         scale_window = keep.tile([P, T], U8, name="scale_window", tag="scale_window", align_bytes=64)
         nc.vector.memset(scale_window[:].bitcast(I32), 0)
-        tab_planes = keep.tile([P, PASSES, S], U8, name="tab_planes", align_bytes=64)
-        nc.vector.memset(tab_planes[:].rearrange("p a n -> p (a n)").bitcast(I32), 0)
+        moved_planes = keep.tile([P, PASSES - 1, S], U8, name="moved_planes", align_bytes=64)
+        nc.vector.memset(moved_planes[:].rearrange("p a n -> p (a n)").bitcast(I32), 0)
         w4_planes = keep.tile([P, PASSES, M], U8, name="w4_planes", align_bytes=64)
         nc.vector.memset(w4_planes[:].rearrange("p a n -> p (a n)").bitcast(I32), 0)
         bias_rows = keep.tile([P, P], F32, name="bias_rows")
@@ -57,7 +56,6 @@ def tile_list_tabgate_silu_kernel(
         make_identity(nc, ident[:])
         warm = keep.tile([P, 1], F32, name="warm")
         nc.scalar.activation(warm[:], ident[:, 0:1], SILU)
-        nc.gpsimd.dma_start(bias_rows[0:N_TILES, :], b.rearrange("(i p) -> i p", p=P))
         for r in range(PACK):
             nc.gpsimd.dma_start(
                 w4_planes[r:P:32, :, :].bitcast(I32),
@@ -86,30 +84,34 @@ def tile_list_tabgate_silu_kernel(
 
         tab_win = [load_tab(0, "tab0")]
         nc.sync.dma_start(offsets[:], offs)
-        for a in range(PASSES):
-            first = ROW0 + 4 * a
-            nc.sync.dma_start(
-                scale_window[first : first + 3 * (SCALE_ROWS - 1) + 1 : 3, :].bitcast(I32),
-                tab_scales[a].bitcast(I32),
-            )
         down_raw = [load_down(0, "down0")]
+        for q in range(4):
+            nc.sync.dma_start(
+                scale_window[32 * q : 32 * q + 4 * PASSES, :].bitcast(I32),
+                tab_scales[:, 4 * q : 4 * q + 4, :].bitcast(I32),
+            )
+        nc.sync.dma_start(bias_rows[0:N_TILES, :], b.rearrange("(i p) -> i p", p=P))
         tab_win.append(load_tab(1, "tab1"))
         down_raw.append(load_down(1, "down1"))
+        down_raw.append(load_down(2, "down2"))
+        tab_win.append(load_tab(2, "tab2"))
         w4_passes = load_w4(0, 1, "w4_first")
 
-        picked_rows = keep.tile([P, S], U8, name="picked_rows", tag="picked_rows", align_bytes=64)
-        nc.vector.tensor_copy(picked_rows[:], scale_window[:].indirect(offsets[:]))
-        for r in range(PACK):
-            first = ROW0 + 3 * r
-            nc.sync.dma_start(
-                tab_planes[r:P:32, :, :].rearrange("p a n -> p (a n)").bitcast(I32),
-                picked_rows[first : first + 4 * (4 * PASSES - 1) + 1 : 4, :].bitcast(I32),
-            )
+        bias_bank = psum.tile([P, HALF], F32, name="bias_bank", tag="bank7")
+        nc.tensor.transpose(bias_bank[:, 0:P], bias_rows[:], ident[:])
+        bias = keep.tile([P, N_TILES], F32, name="bias")
+        nc.scalar.copy(bias[:], bias_bank[:, 0:N_TILES])
 
-        picked = [
-            keep.tile([P, S], U32, name="picked%d" % a, tag="scale_window" if a == 0 else "picked%d" % a, align_bytes=64)
-            for a in range(PASSES)
-        ]
+        picked = [keep.tile([P, S], U32, name="picked%d" % a, align_bytes=64) for a in range(PASSES - 1)]
+        picked_rows = keep.tile([P, S], U8, name="picked_rows", align_bytes=64)
+
+        def move_plane(a):
+            for r in range(PACK):
+                nc.sync.dma_start(
+                    moved_planes[r:P:32, a - 1, :].bitcast(I32),
+                    picked_rows[4 * a + r : P : 32, :].bitcast(I32),
+                )
+
         down_codes = [keep.tile([P, R], U32, name="down_codes%d" % a, tag="down_codes%d" % a, align_bytes=64) for a in range(PASSES)]
         down_scales = [keep.tile([P, R], U8, name="down_scales%d" % a, tag="down_scales%d" % a, align_bytes=64) for a in range(PASSES)]
         h_banks = [psum.tile([P, PACK, CHUNK], F32, name="h_bank%d" % c, tag="bank%d" % c) for c in range(S // CHUNK)]
@@ -141,7 +143,7 @@ def tile_list_tabgate_silu_kernel(
                         lhsT=down_codes[a][:, t * P : (t + 1) * P].bitcast(FP8X4),
                         lhsT_scale=down_scales[a][:, t * P : (t + 1) * P],
                         rhs=picked[a][:, cols].bitcast(FP8X4),
-                        rhs_scale=tab_planes[:, a, cols],
+                        rhs_scale=picked_rows[4 * a : P, cols],
                         start=(a == 0 and t == 0),
                         stop=(a == PASSES - 1 and t == PACK - 1),
                     )
@@ -153,23 +155,24 @@ def tile_list_tabgate_silu_kernel(
             quantize_down(a, 2, high)
 
         pick_words(0, 0, S)
-        down_raw.append(load_down(2, "tab0"))
-        prepare_down(0, nc.scalar.copy)
-        tab_win.append(load_tab(2, "down0"))
-        up_raw = keep.tile([P, PACK, M], F32, name="up_raw", tag="down_bf0_0", align_bytes=64)
+        nc.vector.tensor_copy(picked_rows[:], scale_window[:].indirect(offsets[:]))
+        move_plane(1)
+        up_raw = keep.tile([P, PACK, M], F32, name="up_raw", tag="scale_window", align_bytes=64)
         nc.sync.dma_start(up_raw[:], up.rearrange("(p j) n -> p j n", j=PACK))
+        move_plane(2)
+        prepare_down(0, nc.scalar.copy)
         per_half = HALF // CHUNK
         h_passes(0, 0, 2 * per_half)
-        w4_passes = w4_passes + load_w4(1, PASSES, "down_bf0_2")
+        w4_passes = w4_passes + load_w4(1, PASSES, "down0")
         pick_words(1, 0, S)
         prepare_down(1, nc.vector.tensor_copy)
         gates = [load_gate(0, "down1"), load_gate(1, "down_bf1_0"), load_gate(2, "down_bf1_2")]
         h_passes(1, 0, 2 * per_half)
         prepare_down(2, nc.vector.tensor_copy)
-        gates = gates + [load_gate(3, "tab0"), load_gate(4, "down_bf2_0"), load_gate(5, "down_bf2_2")]
+        picked.append(keep.tile([P, S], U32, name="picked2", tag="down_bf2_2", align_bytes=64))
         for j0 in range(0, S, QUARTER):
             pick_words(PASSES - 1, j0, j0 + QUARTER)
-        gates.append(load_gate(6, "down0"))
+        gates = gates + [load_gate(3, "down2"), load_gate(4, "down_bf2_0"), load_gate(5, "tab2")]
 
         h_bf = [keep.tile([P, HALF, PACK], BF16, name="h_bf%d" % u, tag="h_bf%d" % u, align_bytes=64) for u in range(2)]
         h_codes = {}
@@ -177,19 +180,11 @@ def tile_list_tabgate_silu_kernel(
         for u in range(2):
             h_passes(PASSES - 1, u * per_half, (u + 1) * per_half)
             for c in range(per_half):
-                copy = nc.vector.tensor_copy if u * per_half + c in (3, 5) else nc.scalar.copy
+                copy = nc.vector.tensor_copy if u * per_half + c in (2, 4) else nc.scalar.copy
                 copy(
                     h_bf[u][:, c * CHUNK : (c + 1) * CHUNK, :],
                     h_banks[u * per_half + c][:].rearrange("p t j -> p j t"),
                 )
-        bias_bank = psum.tile([P, HALF], F32, name="bias_bank", tag="bank0")
-        nc.tensor.transpose(bias_bank[:, 0:P], bias_rows[:], ident[:])
-        bias_cols = []
-        for i0, i1 in ((0, 1), (1, N_TILES)):
-            part = keep.tile([P, i1 - i0], F32, name="bias%d" % i0, tag="bias%d" % i0, align_bytes=64)
-            nc.scalar.copy(part[:], bias_bank[:, i0:i1])
-            bias_cols = bias_cols + [part[:, i : i + 1] for i in range(i1 - i0)]
-
 
         def quantize_h(u, tag):
             h_codes[u] = keep.tile([P, HALF], U32, name="h_codes%d" % u, tag=tag, align_bytes=64)
@@ -202,37 +197,44 @@ def tile_list_tabgate_silu_kernel(
         up_codes = {}
         up_scales = keep.tile([P, M], U8, name="up_scales", align_bytes=64)
 
-        def round_up(q, copy, tag):
-            cols = slice(q * QUARTER, (q + 1) * QUARTER)
-            grouped = keep.tile([P, QUARTER, PACK], BF16, name="up_bf%d" % q, tag=tag, align_bytes=64)
+        def round_up(n0, n1, copy, tag):
+            grouped = keep.tile([P, n1 - n0, PACK], BF16, name="up_bf%d" % n0, tag=tag, align_bytes=64)
             copy(
                 grouped[:].rearrange("p (c i) j -> p c j i", i=4),
-                up_raw[:, :, cols].rearrange("p j (c i) -> p c j i", i=4),
+                up_raw[:, :, n0:n1].rearrange("p j (c i) -> p c j i", i=4),
             )
             return grouped
 
-        def quantize_up(q, grouped, tag):
-            up_codes[q] = keep.tile([P, QUARTER], U32, name="up_codes%d" % q, tag=tag, align_bytes=64)
+        def quantize_up(n0, n1, grouped, tag):
+            codes = keep.tile([P, n1 - n0], U32, name="up_codes%d" % n0, tag=tag, align_bytes=64)
             nc.vector.quantize_mx(
-                out=up_codes[q][:].bitcast(FP8X4),
-                scales=up_scales[:, q * QUARTER : (q + 1) * QUARTER],
+                out=codes[:].bitcast(FP8X4),
+                scales=up_scales[:, n0:n1],
                 in_=grouped[:].rearrange("p n j -> p (n j)"),
             )
+            for n in range(n0, n1, P):
+                up_codes[n // P] = codes[:, n - n0 : n - n0 + P]
 
         quantize_h(0, "h_codes0")
-        quantize_up(0, round_up(0, nc.vector.tensor_copy, "h_bf0"), "up_codes0")
+        quantize_up(0, HALF, round_up(0, HALF, nc.vector.tensor_copy, "h_bf0"), "up_codes0")
         quantize_h(1, "h_bf0")
-        quantize_up(1, round_up(1, nc.vector.tensor_copy, "h_bf1"), "up_codes1")
-        quantize_up(2, round_up(2, nc.scalar.copy, "down_codes2"), "up_codes2")
-        gates.append(load_gate(7, "h_bf1"))
+        up_last = round_up(HALF + QUARTER, M, nc.vector.tensor_copy, "h_bf1")
+        up_third = round_up(HALF, HALF + QUARTER, nc.scalar.copy, "down_codes2")
+        quantize_up(HALF, HALF + QUARTER, up_third, "up_codes2")
+        quantize_up(HALF + QUARTER, M, up_last, "up_codes3")
+        gates = gates + [load_gate(6, "h_bf1"), load_gate(7, "scale_window")]
 
+        stores = {0: (4, "tab0"), 4: (2, "tab1"), 6: (1, "results6"), 7: (1, "results7")}
         for i in range(N_TILES):
             rows = slice(i * P, (i + 1) * P)
-            act = work.tile([P, S], F32, name="act%d" % i, tag="act", bufs=4)
+            if i == 0:
+                act = keep.tile([P, S], F32, name="act0", tag="down_codes2", align_bytes=64)
+            else:
+                act = work.tile([P, S], F32, name="act%d" % i, tag="act", bufs=4)
             for u in range(2):
                 cols = slice(u * HALF, (u + 1) * HALF)
                 bank = psum.tile(
-                    [P, HALF], F32, name="y_bank%d_%d" % (i, u), tag="bank%d" % (4 + (2 * i + u) % Y_BANKS)
+                    [P, HALF], F32, name="y_bank%d_%d" % (i, u), tag="bank%d" % ((2 * i + u) % Y_BANKS)
                 )
                 for a in range(PASSES):
                     nc.tensor.matmul_mx(
@@ -240,24 +242,24 @@ def tile_list_tabgate_silu_kernel(
                         lhsT=w4_passes[a][:, 2 * P * i : 2 * P * (i + 1)].bitcast(FP4X4),
                         lhsT_scale=w4_planes[:, a, rows],
                         rhs=picked[a][:, cols].bitcast(FP8X4),
-                        rhs_scale=tab_planes[:, a, cols],
+                        rhs_scale=picked_rows[:, cols] if a == 0 else moved_planes[:, a - 1, cols],
                         start=(a == 0),
                         stop=False,
                     )
                 nc.tensor.matmul_mx(
                     out=bank[:],
-                    lhsT=up_codes[i // 2][:, (i % 2) * P : (i % 2 + 1) * P].bitcast(FP8X4),
+                    lhsT=up_codes[i].bitcast(FP8X4),
                     lhsT_scale=up_scales[:, rows],
                     rhs=h_codes[u][:].bitcast(FP8X4),
                     rhs_scale=h_scales[u][:],
                     start=False,
                     stop=True,
                 )
-                nc.scalar.activation(act[:, cols], bank[:], SILU, bias=bias_cols[i])
-            if i == 0:
-                late_up = round_up(3, nc.scalar.copy, "bias0")
-            tag = "bias0" if i == 3 else "result%d" % i
-            result = keep.tile([P, S], F32, name="result%d" % i, tag=tag, align_bytes=64)
+                nc.scalar.activation(act[:, cols], bank[:], SILU, bias=bias[:, i : i + 1])
+            if i in stores:
+                first = i
+                count, tag = stores[i]
+                results = keep.tile([P, count, S], F32, name="results%d" % i, tag=tag, align_bytes=64)
             if i == 0:
                 cuts = (0, HALF, S)
             elif i == N_TILES - 1:
@@ -265,10 +267,12 @@ def tile_list_tabgate_silu_kernel(
             else:
                 cuts = (0, S)
             for j0, j1 in zip(cuts, cuts[1:]):
-                nc.vector.tensor_tensor(result[:, j0:j1], gates[i][:].indirect(entries(j0, j1)), act[:, j0:j1], MULT)
+                nc.vector.tensor_tensor(
+                    results[:, i - first, j0:j1], gates[i][:].indirect(entries(j0, j1)), act[:, j0:j1], MULT
+                )
                 if i == N_TILES - 1:
-                    nc.sync.dma_start(out[rows, j0:j1], result[:, j0:j1])
-            if i < N_TILES - 1:
-                nc.sync.dma_start(out[rows, :], result[:])
-            if i == 1:
-                quantize_up(3, late_up, "down_bf1_0")
+                    nc.sync.dma_start(out[rows, j0:j1], results[:, 0, j0:j1])
+            if i == first + count - 1 and i < N_TILES - 1:
+                nc.sync.dma_start(
+                    out[first * P : (first + count) * P, :].rearrange("(i p) j -> p i j", p=P), results[:]
+                )

@@ -54,8 +54,6 @@ def tile_list_tabgate_silu_kernel(
         nc.gpsimd.memset(bias_rows[:], 0.0)
         ident = keep.tile([P, P], F32, name="ident")
         make_identity(nc, ident[:])
-        warm = keep.tile([P, 1], F32, name="warm")
-        nc.scalar.activation(warm[:], ident[:, 0:1], SILU)
         for r in range(PACK):
             nc.gpsimd.dma_start(
                 w4_planes[r:P:32, :, :].bitcast(I32),

@@ -27,7 +27,7 @@ QUARTER = 256
 CHUNK = 128
 N_TILES = M // P
 LIST_COLS = 16
-Y_BANKS = 3
+Y_BANKS = 4
 
 
 def tile_list_tabgate_silu_kernel(
@@ -214,8 +214,11 @@ def tile_list_tabgate_silu_kernel(
                 up_codes[n // P] = codes[:, n - n0 : n - n0 + P]
 
         quantize_h(0, "h_codes0")
-        quantize_up(0, HALF, round_up(0, HALF, nc.vector.tensor_copy, "h_bf0"), "up_codes0")
+        up_first = round_up(0, QUARTER, nc.vector.tensor_copy, "h_bf0")
+        up_second = round_up(QUARTER, HALF, nc.vector.tensor_copy, "up_bf1")
+        quantize_up(0, QUARTER, up_first, "up_codes0")
         quantize_h(1, "h_bf0")
+        quantize_up(QUARTER, HALF, up_second, "up_codes1")
         up_last = round_up(HALF + QUARTER, M, nc.vector.tensor_copy, "h_bf1")
         up_third = round_up(HALF, HALF + QUARTER, nc.scalar.copy, "down_codes2")
         quantize_up(HALF, HALF + QUARTER, up_third, "up_codes2")
@@ -225,10 +228,7 @@ def tile_list_tabgate_silu_kernel(
         stores = {0: (4, "tab0"), 4: (2, "tab1"), 6: (1, "results6"), 7: (1, "results7")}
         for i in range(N_TILES):
             rows = slice(i * P, (i + 1) * P)
-            if i == 0:
-                act = keep.tile([P, S], F32, name="act0", tag="down_codes2", align_bytes=64)
-            else:
-                act = work.tile([P, S], F32, name="act%d" % i, tag="act", bufs=4)
+            act = work.tile([P, S], F32, name="act%d" % i, tag="act", bufs=4)
             for u in range(2):
                 cols = slice(u * HALF, (u + 1) * HALF)
                 bank = psum.tile(

@@ -44,11 +44,11 @@ def tile_list_tabgate_silu_kernel(
         def entries(j0, j1):
             return offsets[:, j0 // LIST_COLS : j1 // LIST_COLS]
 
-        scale_window = keep.tile([P, T], U8, name="scale_window", tag="scale_window", align_bytes=64)
+        scale_window = keep.tile([P, T], U8, name="scale_window", tag="scale_window", align_bytes=256)
         nc.vector.memset(scale_window[:].bitcast(I32), 0)
-        moved_planes = keep.tile([P, PASSES - 1, S], U8, name="moved_planes", align_bytes=64)
+        moved_planes = keep.tile([P, PASSES - 1, S], U8, name="moved_planes", align_bytes=256)
         nc.vector.memset(moved_planes[:].rearrange("p a n -> p (a n)").bitcast(I32), 0)
-        w4_planes = keep.tile([P, PASSES, M], U8, name="w4_planes", align_bytes=64)
+        w4_planes = keep.tile([P, PASSES, M], U8, name="w4_planes", align_bytes=256)
         nc.vector.memset(w4_planes[:].rearrange("p a n -> p (a n)").bitcast(I32), 0)
         bias_rows = keep.tile([P, P], F32, name="bias_rows")
         nc.gpsimd.memset(bias_rows[:], 0.0)
@@ -61,22 +61,22 @@ def tile_list_tabgate_silu_kernel(
             )
 
         def load_tab(a, tag):
-            words = keep.tile([P, T], U32, name="tab_words%d" % a, tag=tag, align_bytes=64)
+            words = keep.tile([P, T], U32, name="tab_words%d" % a, tag=tag, align_bytes=256)
             nc.sync.dma_start(words[:].bitcast(I32), tab_words[a].rearrange("p t i -> p (t i)").bitcast(I32))
             return words
 
         def load_down(a, tag):
-            raw = keep.tile([P, PACK, R], F32, name="down_raw%d" % a, tag=tag, align_bytes=64)
+            raw = keep.tile([P, PACK, R], F32, name="down_raw%d" % a, tag=tag, align_bytes=256)
             nc.sync.dma_start(raw[:], down[a * K_PASS : (a + 1) * K_PASS, :].rearrange("(p j) r -> p j r", j=PACK))
             return raw
 
         def load_w4(a0, a1, tag):
-            words = keep.tile([P, a1 - a0, 2 * M], U8, name="w4_words%d" % a0, tag=tag, align_bytes=64)
+            words = keep.tile([P, a1 - a0, 2 * M], U8, name="w4_words%d" % a0, tag=tag, align_bytes=256)
             nc.sync.dma_start(words[:].bitcast(I32), w4_words[a0:a1].rearrange("a p c -> p a c").bitcast(I32))
             return [words[:, a, :] for a in range(a1 - a0)]
 
         def load_gate(i, tag):
-            gate = keep.tile([P, T], F32, name="gate%d" % i, tag=tag, align_bytes=64)
+            gate = keep.tile([P, T], F32, name="gate%d" % i, tag=tag, align_bytes=256)
             nc.sync.dma_start(gate[:], gT[i * P : (i + 1) * P, :])
             return gate
 
@@ -100,8 +100,8 @@ def tile_list_tabgate_silu_kernel(
         bias = keep.tile([P, N_TILES], F32, name="bias")
         nc.scalar.copy(bias[:], bias_bank[:, 0:N_TILES])
 
-        picked = [keep.tile([P, S], U32, name="picked%d" % a, align_bytes=64) for a in range(PASSES - 1)]
-        picked_rows = keep.tile([P, S], U8, name="picked_rows", align_bytes=64)
+        picked = [keep.tile([P, S], U32, name="picked%d" % a, align_bytes=256) for a in range(PASSES - 1)]
+        picked_rows = keep.tile([P, S], U8, name="picked_rows", align_bytes=256)
 
         def move_plane(a):
             for r in range(PACK):
@@ -110,15 +110,15 @@ def tile_list_tabgate_silu_kernel(
                     picked_rows[4 * a + r : P : 32, :].bitcast(I32),
                 )
 
-        down_codes = [keep.tile([P, R], U32, name="down_codes%d" % a, tag="down_codes%d" % a, align_bytes=64) for a in range(PASSES)]
-        down_scales = [keep.tile([P, R], U8, name="down_scales%d" % a, tag="down_scales%d" % a, align_bytes=64) for a in range(PASSES)]
+        down_codes = [keep.tile([P, R], U32, name="down_codes%d" % a, tag="down_codes%d" % a, align_bytes=256) for a in range(PASSES)]
+        down_scales = [keep.tile([P, R], U8, name="down_scales%d" % a, tag="down_scales%d" % a, align_bytes=256) for a in range(PASSES)]
         h_banks = [psum.tile([P, PACK, CHUNK], F32, name="h_bank%d" % c, tag="bank%d" % c) for c in range(S // CHUNK)]
 
         def pick_words(a, j0, j1):
             nc.vector.tensor_copy(picked[a][:, j0:j1], tab_win[a][:].indirect(entries(j0, j1)))
 
         def round_down(a, t0, copy):
-            grouped = keep.tile([P, 2, P, PACK], BF16, name="down_bf%d_%d" % (a, t0), tag="down_bf%d_%d" % (a, t0), align_bytes=64)
+            grouped = keep.tile([P, 2, P, PACK], BF16, name="down_bf%d_%d" % (a, t0), tag="down_bf%d_%d" % (a, t0), align_bytes=256)
             copy(
                 grouped[:].rearrange("p t m j -> p m t j"),
                 down_raw[a][:].rearrange("p j (m t) -> p m t j", t=PACK)[:, :, t0 : t0 + 2, :],
@@ -155,7 +155,7 @@ def tile_list_tabgate_silu_kernel(
         pick_words(0, 0, S)
         nc.vector.tensor_copy(picked_rows[:], scale_window[:].indirect(offsets[:]))
         move_plane(1)
-        up_raw = keep.tile([P, PACK, M], F32, name="up_raw", tag="scale_window", align_bytes=64)
+        up_raw = keep.tile([P, PACK, M], F32, name="up_raw", tag="scale_window", align_bytes=256)
         nc.sync.dma_start(up_raw[:], up.rearrange("(p j) n -> p j n", j=PACK))
         move_plane(2)
         prepare_down(0, nc.scalar.copy)
@@ -167,14 +167,14 @@ def tile_list_tabgate_silu_kernel(
         gates = [load_gate(0, "down1"), load_gate(1, "down_bf1_0"), load_gate(2, "down_bf1_2")]
         h_passes(1, 0, 2 * per_half)
         prepare_down(2, nc.vector.tensor_copy)
-        picked.append(keep.tile([P, S], U32, name="picked2", tag="down_bf2_2", align_bytes=64))
+        picked.append(keep.tile([P, S], U32, name="picked2", tag="down_bf2_2", align_bytes=256))
         for j0 in range(0, S, QUARTER):
             pick_words(PASSES - 1, j0, j0 + QUARTER)
         gates = gates + [load_gate(3, "down2"), load_gate(4, "down_bf2_0"), load_gate(5, "tab2")]
 
-        h_bf = [keep.tile([P, HALF, PACK], BF16, name="h_bf%d" % u, tag="h_bf%d" % u, align_bytes=64) for u in range(2)]
+        h_bf = [keep.tile([P, HALF, PACK], BF16, name="h_bf%d" % u, tag="h_bf%d" % u, align_bytes=256) for u in range(2)]
         h_codes = {}
-        h_scales = [keep.tile([P, HALF], U8, name="h_scales%d" % u, align_bytes=64) for u in range(2)]
+        h_scales = [keep.tile([P, HALF], U8, name="h_scales%d" % u, align_bytes=256) for u in range(2)]
         for u in range(2):
             h_passes(PASSES - 1, u * per_half, (u + 1) * per_half)
             for c in range(per_half):
@@ -185,7 +185,7 @@ def tile_list_tabgate_silu_kernel(
                 )
 
         def quantize_h(u, tag):
-            h_codes[u] = keep.tile([P, HALF], U32, name="h_codes%d" % u, tag=tag, align_bytes=64)
+            h_codes[u] = keep.tile([P, HALF], U32, name="h_codes%d" % u, tag=tag, align_bytes=256)
             nc.vector.quantize_mx(
                 out=h_codes[u][:].bitcast(FP8X4),
                 scales=h_scales[u][:],
@@ -193,10 +193,10 @@ def tile_list_tabgate_silu_kernel(
             )
 
         up_codes = {}
-        up_scales = keep.tile([P, M], U8, name="up_scales", align_bytes=64)
+        up_scales = keep.tile([P, M], U8, name="up_scales", align_bytes=256)
 
         def round_up(n0, n1, copy, tag):
-            grouped = keep.tile([P, n1 - n0, PACK], BF16, name="up_bf%d" % n0, tag=tag, align_bytes=64)
+            grouped = keep.tile([P, n1 - n0, PACK], BF16, name="up_bf%d" % n0, tag=tag, align_bytes=256)
             copy(
                 grouped[:].rearrange("p (c i) j -> p c j i", i=4),
                 up_raw[:, :, n0:n1].rearrange("p j (c i) -> p c j i", i=4),
@@ -204,7 +204,7 @@ def tile_list_tabgate_silu_kernel(
             return grouped
 
         def quantize_up(n0, n1, grouped, tag):
-            codes = keep.tile([P, n1 - n0], U32, name="up_codes%d" % n0, tag=tag, align_bytes=64)
+            codes = keep.tile([P, n1 - n0], U32, name="up_codes%d" % n0, tag=tag, align_bytes=256)
             nc.vector.quantize_mx(
                 out=codes[:].bitcast(FP8X4),
                 scales=up_scales[:, n0:n1],
@@ -257,7 +257,7 @@ def tile_list_tabgate_silu_kernel(
             if i in stores:
                 first = i
                 count, tag = stores[i]
-                results = keep.tile([P, count, S], F32, name="results%d" % i, tag=tag, align_bytes=64)
+                results = keep.tile([P, count, S], F32, name="results%d" % i, tag=tag, align_bytes=256)
             if i == 0:
                 cuts = (0, HALF, S)
             elif i == N_TILES - 1:

from contextlib import ExitStack

import concourse.mybir as mybir
from concourse.masks import make_identity

K, M, T, S, R = 1536, 1024, 2048, 1024, 512
FLOPS = 2 * S * (K * R + K * M + R * M)

F32 = mybir.dt.float32
BF16 = mybir.dt.bfloat16
I32 = mybir.dt.int32
U32 = mybir.dt.uint32
U16 = mybir.dt.uint16
U8 = mybir.dt.uint8
FP8X4 = mybir.dt.float8_e4m3fn_x4
FP4X4 = mybir.dt.float4_e2m1fn_x4
MULT = mybir.AluOpType.mult
SILU = mybir.ActivationFunctionType.Silu

P = 128
PACK = 4
K_PASS = P * PACK
PASSES = K // K_PASS
SCALE_ROWS = 16
HALF = 512
QUARTER = 256
CHUNK = 128
N_TILES = M // P
LIST_COLS = 16
Y_BANKS = 4


def tile_list_tabgate_silu_kernel(
    tc, tab_words, tab_scales, w4_words, w4_scales, down, up, gT, b, offs, out
):
    nc = tc.nc
    with ExitStack() as ctx:
        keep = ctx.enter_context(tc.tile_pool(name="keep", bufs=1))
        work = ctx.enter_context(tc.tile_pool(name="work", bufs=1))
        psum = ctx.enter_context(tc.psum_pool(name="psum", bufs=1))

        offsets = keep.tile([P, S // LIST_COLS], U16, name="offsets")

        def entries(j0, j1):
            return offsets[:, j0 // LIST_COLS : j1 // LIST_COLS]

        scale_window = keep.tile([P, T], U8, name="scale_window", tag="scale_window", align_bytes=256)
        nc.vector.memset(scale_window[:].bitcast(I32), 0)
        moved_planes = keep.tile([P, PASSES - 1, S], U8, name="moved_planes", align_bytes=256)
        nc.vector.memset(moved_planes[:].rearrange("p a n -> p (a n)").bitcast(I32), 0)
        w4_planes = keep.tile([P, PASSES, M], U8, name="w4_planes", align_bytes=256)
        nc.vector.memset(w4_planes[:].rearrange("p a n -> p (a n)").bitcast(I32), 0)
        bias_rows = keep.tile([P, P], F32, name="bias_rows")
        nc.gpsimd.memset(bias_rows[:], 0.0)
        ident = keep.tile([P, P], F32, name="ident")
        make_identity(nc, ident[:])
        for r in range(PACK):
            nc.gpsimd.dma_start(
                w4_planes[r:P:32, :, :].bitcast(I32),
                w4_scales[:, r:SCALE_ROWS:PACK, :].rearrange("a q n -> q a n").bitcast(I32),
            )

        def load_tab(a, tag):
            words = keep.tile([P, T], U32, name="tab_words%d" % a, tag=tag, align_bytes=256)
            nc.sync.dma_start(words[:].bitcast(I32), tab_words[a].rearrange("p t i -> p (t i)").bitcast(I32))
            return words

        def load_down(a, tag):
            raw = keep.tile([P, PACK, R], F32, name="down_raw%d" % a, tag=tag, align_bytes=256)
            nc.sync.dma_start(raw[:], down[a * K_PASS : (a + 1) * K_PASS, :].rearrange("(p j) r -> p j r", j=PACK))
            return raw

        def load_w4(a0, a1, tag):
            words = keep.tile([P, a1 - a0, 2 * M], U8, name="w4_words%d" % a0, tag=tag, align_bytes=256)
            nc.sync.dma_start(words[:].bitcast(I32), w4_words[a0:a1].rearrange("a p c -> p a c").bitcast(I32))
            return [words[:, a, :] for a in range(a1 - a0)]

        def load_gate(i, tag):
            gate = keep.tile([P, T], F32, name="gate%d" % i, tag=tag, align_bytes=256)
            nc.sync.dma_start(gate[:], gT[i * P : (i + 1) * P, :])
            return gate

        tab_win = [load_tab(0, "tab0")]
        nc.sync.dma_start(offsets[:], offs)
        down_raw = [load_down(0, "down0")]
        for q in range(4):
            nc.sync.dma_start(
                scale_window[32 * q : 32 * q + 4 * PASSES, :].bitcast(I32),
                tab_scales[:, 4 * q : 4 * q + 4, :].bitcast(I32),
            )
        nc.sync.dma_start(bias_rows[0:N_TILES, :], b.rearrange("(i p) -> i p", p=P))
        tab_win.append(load_tab(1, "tab1"))
        down_raw.append(load_down(1, "down1"))
        down_raw.append(load_down(2, "down2"))
        tab_win.append(load_tab(2, "tab2"))
        w4_passes = load_w4(0, 1, "w4_first")

        bias_bank = psum.tile([P, HALF], F32, name="bias_bank", tag="bank7")
        nc.tensor.transpose(bias_bank[:, 0:P], bias_rows[:], ident[:])
        bias = keep.tile([P, N_TILES], F32, name="bias")
        nc.scalar.copy(bias[:], bias_bank[:, 0:N_TILES])

        picked = [keep.tile([P, S], U32, name="picked%d" % a, align_bytes=256) for a in range(PASSES - 1)]
        picked_rows = keep.tile([P, S], U8, name="picked_rows", align_bytes=256)

        def move_plane(a):
            for r in range(PACK):
                nc.sync.dma_start(
                    moved_planes[r:P:32, a - 1, :].bitcast(I32),
                    picked_rows[4 * a + r : P : 32, :].bitcast(I32),
                )

        down_codes = [keep.tile([P, R], U32, name="down_codes%d" % a, tag="down_codes%d" % a, align_bytes=256) for a in range(PASSES)]
        down_scales = [keep.tile([P, R], U8, name="down_scales%d" % a, tag="down_scales%d" % a, align_bytes=256) for a in range(PASSES)]
        h_banks = [psum.tile([P, PACK, CHUNK], F32, name="h_bank%d" % c, tag="bank%d" % c) for c in range(S // CHUNK)]

        def pick_words(a, j0, j1):
            nc.vector.tensor_copy(picked[a][:, j0:j1], tab_win[a][:].indirect(entries(j0, j1)))

        def round_down(a, t0, copy):
            grouped = keep.tile([P, 2, P, PACK], BF16, name="down_bf%d_%d" % (a, t0), tag="down_bf%d_%d" % (a, t0), align_bytes=256)
            copy(
                grouped[:].rearrange("p t m j -> p m t j"),
                down_raw[a][:].rearrange("p j (m t) -> p m t j", t=PACK)[:, :, t0 : t0 + 2, :],
            )
            return grouped

        def quantize_down(a, t0, grouped):
            nc.vector.quantize_mx(
                out=down_codes[a][:, t0 * P : (t0 + 2) * P].bitcast(FP8X4),
                scales=down_scales[a][:, t0 * P : (t0 + 2) * P],
                in_=grouped[:].rearrange("p t m j -> p (t m j)"),
            )

        def h_passes(a, c0, c1):
            for c in range(c0, c1):
                cols = slice(c * CHUNK, (c + 1) * CHUNK)
                for t in range(PACK):
                    nc.tensor.matmul_mx(
                        out=h_banks[c][:, t, :],
                        lhsT=down_codes[a][:, t * P : (t + 1) * P].bitcast(FP8X4),
                        lhsT_scale=down_scales[a][:, t * P : (t + 1) * P],
                        rhs=picked[a][:, cols].bitcast(FP8X4),
                        rhs_scale=picked_rows[4 * a : P, cols],
                        start=(a == 0 and t == 0),
                        stop=(a == PASSES - 1 and t == PACK - 1),
                    )

        def prepare_down(a, second_copy):
            low = round_down(a, 0, nc.scalar.copy)
            high = round_down(a, 2, second_copy)
            quantize_down(a, 0, low)
            quantize_down(a, 2, high)

        pick_words(0, 0, S)
        nc.vector.tensor_copy(picked_rows[:], scale_window[:].indirect(offsets[:]))
        move_plane(1)
        up_raw = keep.tile([P, PACK, M], F32, name="up_raw", tag="scale_window", align_bytes=256)
        nc.sync.dma_start(up_raw[:], up.rearrange("(p j) n -> p j n", j=PACK))
        move_plane(2)
        prepare_down(0, nc.scalar.copy)
        per_half = HALF // CHUNK
        h_passes(0, 0, 2 * per_half)
        w4_passes = w4_passes + load_w4(1, PASSES, "down0")
        pick_words(1, 0, S)
        prepare_down(1, nc.vector.tensor_copy)
        gates = [load_gate(0, "down1"), load_gate(1, "down_bf1_0"), load_gate(2, "down_bf1_2")]
        h_passes(1, 0, 2 * per_half)
        prepare_down(2, nc.vector.tensor_copy)
        picked.append(keep.tile([P, S], U32, name="picked2", tag="down_bf2_2", align_bytes=256))
        for j0 in range(0, S, QUARTER):
            pick_words(PASSES - 1, j0, j0 + QUARTER)
        gates = gates + [load_gate(3, "down2"), load_gate(4, "down_bf2_0"), load_gate(5, "tab2")]

        h_bf = [keep.tile([P, HALF, PACK], BF16, name="h_bf%d" % u, tag="h_bf%d" % u, align_bytes=256) for u in range(2)]
        h_codes = {}
        h_scales = [keep.tile([P, HALF], U8, name="h_scales%d" % u, align_bytes=256) for u in range(2)]
        for u in range(2):
            h_passes(PASSES - 1, u * per_half, (u + 1) * per_half)
            for c in range(per_half):
                copy = nc.vector.tensor_copy if u * per_half + c in (2, 4) else nc.scalar.copy
                copy(
                    h_bf[u][:, c * CHUNK : (c + 1) * CHUNK, :],
                    h_banks[u * per_half + c][:].rearrange("p t j -> p j t"),
                )

        def quantize_h(u, tag):
            h_codes[u] = keep.tile([P, HALF], U32, name="h_codes%d" % u, tag=tag, align_bytes=256)
            nc.vector.quantize_mx(
                out=h_codes[u][:].bitcast(FP8X4),
                scales=h_scales[u][:],
                in_=h_bf[u][:].rearrange("p n j -> p (n j)"),
            )

        up_codes = {}
        up_scales = keep.tile([P, M], U8, name="up_scales", align_bytes=256)

        def round_up(n0, n1, copy, tag):
            grouped = keep.tile([P, n1 - n0, PACK], BF16, name="up_bf%d" % n0, tag=tag, align_bytes=256)
            copy(
                grouped[:].rearrange("p (c i) j -> p c j i", i=4),
                up_raw[:, :, n0:n1].rearrange("p j (c i) -> p c j i", i=4),
            )
            return grouped

        def quantize_up(n0, n1, grouped, tag):
            codes = keep.tile([P, n1 - n0], U32, name="up_codes%d" % n0, tag=tag, align_bytes=256)
            nc.vector.quantize_mx(
                out=codes[:].bitcast(FP8X4),
                scales=up_scales[:, n0:n1],
                in_=grouped[:].rearrange("p n j -> p (n j)"),
            )
            for n in range(n0, n1, P):
                up_codes[n // P] = codes[:, n - n0 : n - n0 + P]

        quantize_h(0, "h_codes0")
        up_first = round_up(0, QUARTER, nc.vector.tensor_copy, "h_bf0")
        up_second = round_up(QUARTER, HALF, nc.vector.tensor_copy, "up_bf1")
        quantize_up(0, QUARTER, up_first, "up_codes0")
        quantize_h(1, "h_bf0")
        quantize_up(QUARTER, HALF, up_second, "up_codes1")
        up_last = round_up(HALF + QUARTER, M, nc.vector.tensor_copy, "h_bf1")
        up_third = round_up(HALF, HALF + QUARTER, nc.scalar.copy, "down_codes2")
        quantize_up(HALF, HALF + QUARTER, up_third, "up_codes2")
        quantize_up(HALF + QUARTER, M, up_last, "up_codes3")
        gates = gates + [load_gate(6, "h_bf1"), load_gate(7, "scale_window")]

        stores = {0: (4, "tab0"), 4: (2, "tab1"), 6: (1, "results6"), 7: (1, "results7")}
        for i in range(N_TILES):
            rows = slice(i * P, (i + 1) * P)
            act = work.tile([P, S], F32, name="act%d" % i, tag="act", bufs=4)
            for u in range(2):
                cols = slice(u * HALF, (u + 1) * HALF)
                bank = psum.tile(
                    [P, HALF], F32, name="y_bank%d_%d" % (i, u), tag="bank%d" % ((2 * i + u) % Y_BANKS)
                )
                for a in range(PASSES):
                    nc.tensor.matmul_mx(
                        out=bank[:],
                        lhsT=w4_passes[a][:, 2 * P * i : 2 * P * (i + 1)].bitcast(FP4X4),
                        lhsT_scale=w4_planes[:, a, rows],
                        rhs=picked[a][:, cols].bitcast(FP8X4),
                        rhs_scale=picked_rows[:, cols] if a == 0 else moved_planes[:, a - 1, cols],
                        start=(a == 0),
                        stop=False,
                    )
                nc.tensor.matmul_mx(
                    out=bank[:],
                    lhsT=up_codes[i].bitcast(FP8X4),
                    lhsT_scale=up_scales[:, rows],
                    rhs=h_codes[u][:].bitcast(FP8X4),
                    rhs_scale=h_scales[u][:],
                    start=False,
                    stop=True,
                )
                nc.scalar.activation(act[:, cols], bank[:], SILU, bias=bias[:, i : i + 1])
            if i in stores:
                first = i
                count, tag = stores[i]
                results = keep.tile([P, count, S], F32, name="results%d" % i, tag=tag, align_bytes=256)
            if i == 0:
                cuts = (0, HALF, S)
            elif i == N_TILES - 1:
                cuts = (0, HALF, HALF + QUARTER, S)
            else:
                cuts = (0, S)
            for j0, j1 in zip(cuts, cuts[1:]):
                nc.vector.tensor_tensor(
                    results[:, i - first, j0:j1], gates[i][:].indirect(entries(j0, j1)), act[:, j0:j1], MULT
                )
                if i == N_TILES - 1:
                    nc.sync.dma_start(out[rows, j0:j1], results[:, 0, j0:j1])
            if i == first + count - 1 and i < N_TILES - 1:
                nc.sync.dma_start(
                    out[first * P : (first + count) * P, :].rearrange("(i p) j -> p i j", p=P), results[:]
                )
